import numpy as np
import ml_dtypes


def mxq(x, axis, fmt="e4m3"):
    dtype, down = {"e4m3": (ml_dtypes.float8_e4m3fn, 7), "e5m2": (ml_dtypes.float8_e5m2, 14)}[fmt]
    v = np.moveaxis(np.asarray(x, np.float32).astype(ml_dtypes.bfloat16).astype(np.float64), axis, -1)
    blocks = v.reshape(v.shape[:-1] + (-1, 32))
    amax = np.abs(blocks).max(-1, keepdims=True)
    byte = np.maximum(np.where(amax > 0, np.frexp(amax)[1] - 1 + 127, 0) - down, 1)
    scale = np.exp2(byte - 127.0)
    codes = (blocks / scale).astype(np.float32).astype(dtype).astype(np.float64)
    return np.moveaxis((codes * scale).reshape(v.shape), -1, axis)


WIDE = False


def mx_kscale(k):
    if not WIDE:
        return np.ones(k)
    levels = np.array([10, -10, 5, -5, 0])
    if k % 512:
        return np.exp2(np.random.permutation(np.resize(levels, k // 32))).repeat(32)
    a = np.empty((k // 512, 16))
    for p in range(k // 512):
        a[p, :8] = np.random.permutation(np.resize(levels, 8))
        for g in range(8):
            far = levels[np.abs(levels - a[p, g]) >= 10]
            a[p, g + 8] = far[np.random.randint(len(far))]
    return np.exp2(a.ravel()).repeat(32)


def f64(x):
    return np.asarray(x).astype(np.float64)


def striped(idx):
    return np.tile(idx.reshape(-1, 16).T, (8, 1)).astype(np.uint16)


def unstriped(offs):
    return offs[:16].T.reshape(-1).astype(np.int64)


E2M1 = np.array([0.0, 0.5, 1.0, 1.5, 2.0, 3.0, 4.0, 6.0, -0.0, -0.5, -1.0, -1.5, -2.0, -3.0, -4.0, -6.0])


def pack_weight(w, fmt):
    k, n = w.shape
    w = f64(np.asarray(w, np.float32).astype(ml_dtypes.bfloat16)).reshape(k // 32, 32, n)
    amax = np.abs(w).max(1)
    if fmt == "e4m3":
        byte = np.frexp(amax)[1] - 1 + 127 - 7
    else:
        mant, ex = np.frexp(amax / 6.0)
        byte = np.where(mant > 0.5, ex, ex - 1) + 127
    byte = np.clip(np.where(amax > 0, byte, 1), 1, 254)
    scaled = (w * np.exp2(127.0 - byte)[:, None, :]).reshape(k, n).astype(np.float32)
    by_word = np.ascontiguousarray(scaled.reshape(k // 512, 128, 4, n).transpose(0, 1, 3, 2))
    if fmt == "e4m3":
        words = by_word.astype(ml_dtypes.float8_e4m3fn).view(np.uint8)
    else:
        c = by_word.astype(ml_dtypes.float4_e2m1fn).view(np.uint8) & 0xF
        words = (c[..., 0::2] | (c[..., 1::2] << 4)).reshape(k // 512, 128, 2 * n)
    return np.ascontiguousarray(words), np.ascontiguousarray(byte.astype(np.uint8).reshape(k // 512, 16, n))


def unpack_weight(words, scales, fmt):
    g, _, n = scales.shape
    words = np.ascontiguousarray(words).reshape(g, 128, n, -1)
    if fmt == "e4m3":
        vals = words.view(ml_dtypes.float8_e4m3fn).astype(np.float64)
    else:
        nib = np.empty((g, 128, n, 4), np.uint8)
        nib[..., 0::2] = words & 0xF
        nib[..., 1::2] = words >> 4
        vals = E2M1[nib]
    vals = vals * np.repeat(np.exp2(scales.astype(np.float64) - 127.0), 8, axis=1)[..., None]
    return vals.transpose(0, 1, 3, 2).reshape(g * 512, n)


def gelu(v):
    return 0.5 * v * (1.0 + np.tanh(np.sqrt(2.0 / np.pi) * (v + 0.044715 * v**3)))


K, T, E, C, H, N = 1024, 768, 8, 128, 512, 128
TOP = 3
PAD = 64


def by_expert(wq, xq):
    return np.concatenate([wq[e].T @ xq[:, e * C:(e + 1) * C] for e in range(E)], axis=1)


def setup_inputs():
    n = np.random.standard_normal
    s = mx_kscale(K)[:, None]
    u = mx_kscale(H)
    slot_token = np.empty(E * C, np.int64); pos = np.tile(E * C + np.arange(T) % PAD, (TOP, 1)); taken = np.zeros(T, np.int64)
    liked = np.random.randn(T)
    for e in np.random.permutation(E):
        free = np.flatnonzero(taken < TOP); pick = np.random.permutation(free[np.argsort(-(liked[free] + np.random.gumbel(size=free.size)))[:C]]); slot_token[e * C:(e + 1) * C] = pick
        pos[taken[pick], pick] = e * C + np.arange(C); taken[pick] += 1
    g = np.random.uniform(0.2, 0.8, (TOP, T))
    w1 = [pack_weight(m, "e2m1") for m in n((E, K, H)) / np.sqrt(K) / s[None]]
    w3 = [pack_weight(m, "e2m1") for m in n((E, K, H)) / np.sqrt(K) / s[None] * u[None, None, :]]
    w2 = [pack_weight(m, "e2m1") for m in n((E, H, N)) / np.sqrt(H) / u[None, :, None]]
    x = pack_weight(n((K, T)) * s, "e4m3")
    return {
        "x_words": x[0],
        "x_scales": x[1],
        "w1_words": np.stack([m[0] for m in w1]),
        "w1_scales": np.stack([m[1] for m in w1]),
        "w3_words": np.stack([m[0] for m in w3]),
        "w3_scales": np.stack([m[1] for m in w3]),
        "w2_words": np.stack([m[0] for m in w2]),
        "w2_scales": np.stack([m[1] for m in w2]),
        "gate": np.stack([np.tile(r, (N, 1)) for r in g]).astype(np.float32),
        "offs": striped(slot_token),
        "pos1": striped(pos[0]),
        "pos2": striped(pos[1]),
        "pos3": striped(pos[2]),
    }


def reference(x_words, x_scales, w1_words, w1_scales, w3_words, w3_scales, w2_words, w2_scales, gate, offs, pos1, pos2, pos3):
    idx = unstriped(offs)
    w1 = np.stack([unpack_weight(w1_words[e], w1_scales[e], "e2m1") for e in range(E)])
    w3 = np.stack([unpack_weight(w3_words[e], w3_scales[e], "e2m1") for e in range(E)])
    w2 = np.stack([unpack_weight(w2_words[e], w2_scales[e], "e2m1") for e in range(E)])
    xq = unpack_weight(x_words, x_scales, "e4m3")[:, idx]
    h = gelu(by_expert(w1, xq))
    h = h * by_expert(w3, xq)
    y = by_expert(w2, mxq(h, 0, "e4m3"))
    y = np.concatenate([y, np.zeros((N, PAD))], axis=1)
    return sum(f64(gate[r]) * y[:, unstriped(p)] for r, p in enumerate((pos1, pos2, pos3)))

@@ -1,0 +1,165 @@
+from contextlib import ExitStack
+
+import concourse.mybir as mybir
+from concourse.masks import make_identity
+
+K, T, E, C, H, N = 1024, 768, 8, 128, 512, 128
+TOP = 3
+PAD = 64
+SLOTS = E * C
+P = 128
+PASSES = K // 512
+FLOPS = 2 * SLOTS * (2 * K * H + H * N)
+
+F32 = mybir.dt.float32
+BF16 = mybir.dt.bfloat16
+I32 = mybir.dt.int32
+U32 = mybir.dt.uint32
+U16 = mybir.dt.uint16
+U8 = mybir.dt.uint8
+FP8X4 = mybir.dt.float8_e4m3fn_x4
+FP4X4 = mybir.dt.float4_e2m1fn_x4
+MULT = mybir.AluOpType.mult
+ADD = mybir.AluOpType.add
+GELU = mybir.ActivationFunctionType.Gelu_apprx_tanh
+
+GATHER = 512
+GROUPS = ((0, 1), (2, 3), (4, 5), (6,), (7,))
+CHUNKS = ((0, 512), (512, 768))
+
+
+def load_scale_rows(nc, plane, rows):
+    by_j = rows.rearrange("g (q j) w -> j q g w", j=4)
+    for j in range(4):
+        nc.sync.dma_start(out=plane[j:P:32, :, :].bitcast(I32), in_=by_j[j].bitcast(I32))
+
+
+def tile_moe_ecr_glu_gelu_kernel(tc, x_words, x_scales, w1_words, w1_scales, w3_words, w3_scales, w2_words, w2_scales, gate, offs, pos1, pos2, pos3, out):
+    nc = tc.nc
+    with ExitStack() as ctx:
+        held = ctx.enter_context(tc.tile_pool(name="held", bufs=1))
+        ring = ctx.enter_context(tc.tile_pool(name="ring", bufs=2))
+        psum = ctx.enter_context(tc.psum_pool(name="psum", bufs=2))
+
+        x_plane = held.tile([P, PASSES, T], U8, name="x_plane", align_bytes=64)
+        w1_plane = held.tile([P, E * PASSES, H], U8, name="w1_plane", align_bytes=64)
+        w3_plane = held.tile([P, E * PASSES, H], U8, name="w3_plane", align_bytes=64)
+        w2_plane = held.tile([P, E, N], U8, name="w2_plane", align_bytes=64)
+        for plane in (x_plane, w1_plane, w3_plane, w2_plane):
+            nc.vector.memset(plane[:].bitcast(I32), 0)
+
+        slot_list = held.tile([P, SLOTS // 16], U16, name="slot_list")
+        nc.sync.dma_start(slot_list[:], offs)
+        x_word = [held.tile([P, T], U32, name=f"x_word{s}", align_bytes=64) for s in range(PASSES)]
+        for s in range(PASSES):
+            nc.sync.dma_start(out=x_word[s][:].bitcast(I32), in_=x_words[s].rearrange("p t r -> p (t r)").bitcast(I32))
+        load_scale_rows(nc, x_plane, x_scales)
+        load_scale_rows(nc, w1_plane, w1_scales.rearrange("e s q i -> (e s) q i"))
+        load_scale_rows(nc, w3_plane, w3_scales.rearrange("e s q i -> (e s) q i"))
+        load_scale_rows(nc, w2_plane, w2_scales.rearrange("e s q n -> (e s) q n"))
+
+        w2 = held.tile([P, E, 2 * N], U8, name="w2", align_bytes=64)
+        w1 = [held.tile([P, PASSES, 2 * H], U8, name=f"w1_{e}", align_bytes=64) for e in range(E)]
+        w3 = [held.tile([P, PASSES, 2 * H], U8, name=f"w3_{e}", align_bytes=64) for e in range(E)]
+        for e in range(E):
+            nc.sync.dma_start(out=w1[e][:].bitcast(I32), in_=w1_words[e].rearrange("s p b -> p s b").bitcast(I32))
+            nc.sync.dma_start(out=w3[e][:].bitcast(I32), in_=w3_words[e].rearrange("s p b -> p s b").bitcast(I32))
+            if e == 1:
+                nc.sync.dma_start(out=w2[:].bitcast(I32), in_=w2_words.rearrange("e s p b -> p (e s) b").bitcast(I32))
+
+        token_lists = []
+        for r, pos in enumerate((pos1, pos2, pos3)):
+            token_list = held.tile([P, T // 16], U16, name=f"token_list{r}")
+            nc.sync.dma_start(token_list[:], pos)
+            token_lists.append(token_list)
+        gates = [held.tile([P, T], F32, name=f"gate{r}") for r in range(TOP)]
+        for r in range(TOP):
+            nc.sync.dma_start(out=gates[r][:], in_=gate[r])
+
+        identity = held.tile([P, P], F32, name="identity")
+        make_identity(nc, identity[:])
+        y = held.tile([P, SLOTS + PAD], F32, name="y")
+        nc.vector.memset(y[:, SLOTS:], 0.0)
+
+        pieces = SLOTS // GATHER
+        slot_word = [[held.tile([P, GATHER], U32, name=f"slot_word{g}_{s}", align_bytes=64) for s in range(PASSES)] for g in range(pieces)]
+        slot_plane = [[held.tile([P, GATHER], U8, name=f"slot_plane{g}_{s}", align_bytes=64) for s in range(PASSES)] for g in range(pieces)]
+        for g in range(pieces):
+            offsets = slot_list[:, g * GATHER // 16 : (g + 1) * GATHER // 16]
+            for s in range(PASSES):
+                nc.vector.tensor_copy(slot_word[g][s][:], x_word[s][:].indirect(offsets))
+            for s in range(PASSES):
+                nc.vector.tensor_copy(slot_plane[g][s][:], x_plane[:, s, :].indirect(offsets))
+
+        def first_product(e, words, plane, tag):
+            g, c0 = divmod(e * C, GATHER)
+            acc = psum.tile([P, H], F32, name=tag)
+            for s in range(PASSES):
+                nc.tensor.matmul_mx(
+                    out=acc[:],
+                    lhsT=slot_word[g][s][:, c0 : c0 + C].bitcast(FP8X4),
+                    lhsT_scale=slot_plane[g][s][:, c0 : c0 + C],
+                    rhs=words[:, s, :].bitcast(FP4X4),
+                    rhs_scale=plane[:, e * PASSES + s, :],
+                    start=(s == 0),
+                    stop=(s == PASSES - 1),
+                )
+            return acc[:].rearrange("c (p u v) -> c u p v", u=2, v=2)
+
+        def hidden(e):
+            a = first_product(e, w1[e], w1_plane, "a_sum")
+            b = first_product(e, w3[e], w3_plane, "b_sum")
+            act = ring.tile([P, 2, P, 2], F32, name="act")
+            nc.scalar.activation(out=act[:], in_=a, func=GELU)
+            h = ring.tile([P, 2, P, 2], BF16, name="h", bufs=4)
+            nc.vector.tensor_tensor(out=h[:], in0=b, in1=act[:], op=MULT)
+            return h
+
+        def second(group, hs):
+            width = len(group) * C
+            turned = psum.tile([P, len(group), 2, C], F32, name="turned")
+            for m, h in enumerate(hs):
+                pairs = h[:].rearrange("c u p v -> c (u p v)").bitcast(F32)
+                for u in range(2):
+                    nc.tensor.transpose(turned[:, m, u, :], pairs[:, u * P : (u + 1) * P], identity[:])
+            grouped = ring.tile([P, 4 * width], BF16, name="grouped", align_bytes=64)
+            nc.scalar.copy(
+                out=grouped[:].bitcast(F32).rearrange("p (m c u) -> p m c u", c=C, u=2),
+                in_=turned[:].rearrange("p m u c -> p m c u"),
+            )
+            h_word = ring.tile([P, width], U32, name="h_word", align_bytes=64)
+            h_plane = ring.tile([P, width], U8, name="h_plane", align_bytes=64)
+            nc.vector.quantize_mx(out=h_word[:].bitcast(FP8X4), scales=h_plane[:], in_=grouped[:])
+            y_sum = psum.tile([P, width], F32, name="y_sum")
+            for m, e in enumerate(group):
+                cols = slice(m * C, (m + 1) * C)
+                nc.tensor.matmul_mx(
+                    out=y_sum[:, cols],
+                    lhsT=w2[:, e, :].bitcast(FP4X4),
+                    lhsT_scale=w2_plane[:, e, :],
+                    rhs=h_word[:, cols].bitcast(FP8X4),
+                    rhs_scale=h_plane[:, cols],
+                    start=True,
+                    stop=True,
+                )
+            nc.scalar.copy(out=y[:, group[0] * C : group[0] * C + width], in_=y_sum[:])
+
+        made = [hidden(e) for e in GROUPS[0]]
+        for before, group in zip(GROUPS, GROUPS[1:]):
+            ready = made
+            made = [hidden(e) for e in group]
+            second(before, ready)
+        second(GROUPS[-1], made)
+
+        for t0, t1 in CHUNKS:
+            terms = []
+            for r in range(TOP):
+                term = held.tile([P, t1 - t0], F32, name=f"term{t0}_{r}")
+                nc.vector.tensor_tensor(term[:], y[:].indirect(token_lists[r][:, t0 // 16 : t1 // 16]), gates[r][:, t0:t1], MULT)
+                terms.append(term)
+                if r == 1:
+                    both = held.tile([P, t1 - t0], F32, name=f"both{t0}")
+                    nc.vector.tensor_tensor(both[:], terms[0][:], terms[1][:], ADD)
+            result = held.tile([P, t1 - t0], F32, name=f"result{t0}")
+            nc.vector.tensor_tensor(result[:], both[:], terms[2][:], ADD)
+            nc.sync.dma_start(out=out[:, t0:t1], in_=result[:])

@@ -23,8 +23,8 @@ MULT = mybir.AluOpType.mult
 ADD = mybir.AluOpType.add
 GELU = mybir.ActivationFunctionType.Gelu_apprx_tanh
 
-GATHER = 512
-GROUPS = ((0, 1), (2, 3), (4, 5), (6,), (7,))
+GATHER = 256
+HALF = E // 2
 CHUNKS = ((0, 512), (512, 768))
 
 
@@ -39,33 +39,45 @@ def tile_moe_ecr_glu_gelu_kernel(tc, x_words, x_scales, w1_words, w1_scales, w3_
     with ExitStack() as ctx:
         held = ctx.enter_context(tc.tile_pool(name="held", bufs=1))
         ring = ctx.enter_context(tc.tile_pool(name="ring", bufs=2))
-        psum = ctx.enter_context(tc.psum_pool(name="psum", bufs=2))
+        psum = ctx.enter_context(tc.psum_pool(name="psum", bufs=1))
 
         x_plane = held.tile([P, PASSES, T], U8, name="x_plane", align_bytes=64)
-        w1_plane = held.tile([P, E * PASSES, H], U8, name="w1_plane", align_bytes=64)
-        w3_plane = held.tile([P, E * PASSES, H], U8, name="w3_plane", align_bytes=64)
+        nc.gpsimd.memset(x_plane[:].bitcast(I32), 0)
+        w1_plane = [held.tile([P, HALF * PASSES, H], U8, name=f"w1_plane{g}", align_bytes=64) for g in range(2)]
+        w3_plane = [held.tile([P, HALF * PASSES, H], U8, name=f"w3_plane{g}", align_bytes=64) for g in range(2)]
         w2_plane = held.tile([P, E, N], U8, name="w2_plane", align_bytes=64)
-        for plane in (x_plane, w1_plane, w3_plane, w2_plane):
+        for plane in (w1_plane[0], w3_plane[0], w1_plane[1], w3_plane[1], w2_plane):
             nc.vector.memset(plane[:].bitcast(I32), 0)
 
         slot_list = held.tile([P, SLOTS // 16], U16, name="slot_list")
         nc.sync.dma_start(slot_list[:], offs)
         x_word = [held.tile([P, T], U32, name=f"x_word{s}", align_bytes=64) for s in range(PASSES)]
-        for s in range(PASSES):
-            nc.sync.dma_start(out=x_word[s][:].bitcast(I32), in_=x_words[s].rearrange("p t r -> p (t r)").bitcast(I32))
+        nc.sync.dma_start(out=x_word[0][:].bitcast(I32), in_=x_words[0].rearrange("p t r -> p (t r)").bitcast(I32))
+        nc.sync.dma_start(out=x_word[1][:].bitcast(I32), in_=x_words[1].rearrange("p t r -> p (t r)").bitcast(I32))
         load_scale_rows(nc, x_plane, x_scales)
-        load_scale_rows(nc, w1_plane, w1_scales.rearrange("e s q i -> (e s) q i"))
-        load_scale_rows(nc, w3_plane, w3_scales.rearrange("e s q i -> (e s) q i"))
-        load_scale_rows(nc, w2_plane, w2_scales.rearrange("e s q n -> (e s) q n"))
 
         w2 = held.tile([P, E, 2 * N], U8, name="w2", align_bytes=64)
-        w1 = [held.tile([P, PASSES, 2 * H], U8, name=f"w1_{e}", align_bytes=64) for e in range(E)]
-        w3 = [held.tile([P, PASSES, 2 * H], U8, name=f"w3_{e}", align_bytes=64) for e in range(E)]
+        w1, w3 = {}, {}
+
+        def load_words(words, e, name):
+            tile = held.tile([P, PASSES, 2 * H], U8, name=f"{name}_{e}", align_bytes=64)
+            nc.sync.dma_start(out=tile[:].bitcast(I32), in_=words[e].rearrange("s p b -> p s b").bitcast(I32))
+            return tile
+
+        def load_half(planes, scales, g):
+            load_scale_rows(nc, planes[g], scales[g * HALF : (g + 1) * HALF].rearrange("e s q i -> (e s) q i"))
+
         for e in range(E):
-            nc.sync.dma_start(out=w1[e][:].bitcast(I32), in_=w1_words[e].rearrange("s p b -> p s b").bitcast(I32))
-            nc.sync.dma_start(out=w3[e][:].bitcast(I32), in_=w3_words[e].rearrange("s p b -> p s b").bitcast(I32))
-            if e == 1:
-                nc.sync.dma_start(out=w2[:].bitcast(I32), in_=w2_words.rearrange("e s p b -> p (e s) b").bitcast(I32))
+            g, place = divmod(e, HALF)
+            if place == 0:
+                load_half(w1_plane, w1_scales, g)
+            w1[e] = load_words(w1_words, e, "w1")
+            if place == 0:
+                load_half(w3_plane, w3_scales, g)
+            if e == HALF:
+                load_scale_rows(nc, w2_plane, w2_scales.rearrange("e s q n -> (e s) q n"))
+            w3[e] = load_words(w3_words, e, "w3")
+        nc.sync.dma_start(out=w2[:].bitcast(I32), in_=w2_words.rearrange("e s p b -> p (e s) b").bitcast(I32))
 
         token_lists = []
         for r, pos in enumerate((pos1, pos2, pos3)):
@@ -81,75 +93,96 @@ def tile_moe_ecr_glu_gelu_kernel(tc, x_words, x_scales, w1_words, w1_scales, w3_
         y = held.tile([P, SLOTS + PAD], F32, name="y")
         nc.vector.memset(y[:, SLOTS:], 0.0)
 
-        pieces = SLOTS // GATHER
-        slot_word = [[held.tile([P, GATHER], U32, name=f"slot_word{g}_{s}", align_bytes=64) for s in range(PASSES)] for g in range(pieces)]
-        slot_plane = [[held.tile([P, GATHER], U8, name=f"slot_plane{g}_{s}", align_bytes=64) for s in range(PASSES)] for g in range(pieces)]
-        for g in range(pieces):
-            offsets = slot_list[:, g * GATHER // 16 : (g + 1) * GATHER // 16]
-            for s in range(PASSES):
-                nc.vector.tensor_copy(slot_word[g][s][:], x_word[s][:].indirect(offsets))
-            for s in range(PASSES):
-                nc.vector.tensor_copy(slot_plane[g][s][:], x_plane[:, s, :].indirect(offsets))
+        banks = [psum.tile([P, H], F32, name=f"bank{b}") for b in range(8)]
+        slot_word, slot_plane = {}, {}
 
-        def first_product(e, words, plane, tag):
+        def gather(g):
+            offsets = slot_list[:, g * GATHER // 16 : (g + 1) * GATHER // 16]
+            slot_word[g], slot_plane[g] = [], []
+            for s in range(PASSES):
+                words = ring.tile([P, GATHER], U32, name=f"slot_word{s}", align_bytes=64)
+                nc.vector.tensor_copy(words[:], x_word[s][:].indirect(offsets))
+                plane = ring.tile([P, GATHER], U8, name=f"slot_plane{s}", align_bytes=64, bufs=3)
+                nc.vector.tensor_copy(plane[:], x_plane[:, s, :].indirect(offsets))
+                slot_word[g].append(words)
+                slot_plane[g].append(plane)
+
+        def first_product(e, words, plane, acc):
             g, c0 = divmod(e * C, GATHER)
-            acc = psum.tile([P, H], F32, name=tag)
             for s in range(PASSES):
                 nc.tensor.matmul_mx(
                     out=acc[:],
                     lhsT=slot_word[g][s][:, c0 : c0 + C].bitcast(FP8X4),
                     lhsT_scale=slot_plane[g][s][:, c0 : c0 + C],
                     rhs=words[:, s, :].bitcast(FP4X4),
-                    rhs_scale=plane[:, e * PASSES + s, :],
+                    rhs_scale=plane[e // HALF][:, e % HALF * PASSES + s, :],
                     start=(s == 0),
                     stop=(s == PASSES - 1),
                 )
             return acc[:].rearrange("c (p u v) -> c u p v", u=2, v=2)
 
         def hidden(e):
-            a = first_product(e, w1[e], w1_plane, "a_sum")
-            b = first_product(e, w3[e], w3_plane, "b_sum")
-            act = ring.tile([P, 2, P, 2], F32, name="act")
+            a = first_product(e, w1[e], w1_plane, banks[e % 2])
+            b = first_product(e, w3[e], w3_plane, banks[2 + e % 5])
+            act = ring.tile([P, 2, P, 2], F32, name="act", bufs=5)
             nc.scalar.activation(out=act[:], in_=a, func=GELU)
-            h = ring.tile([P, 2, P, 2], BF16, name="h", bufs=4)
+            h = ring.tile([P, 2, P, 2], BF16, name="h", bufs=8)
             nc.vector.tensor_tensor(out=h[:], in0=b, in1=act[:], op=MULT)
-            return h
+            hs[e] = h
 
-        def second(group, hs):
+        def turn(group, bank):
             width = len(group) * C
-            turned = psum.tile([P, len(group), 2, C], F32, name="turned")
-            for m, h in enumerate(hs):
-                pairs = h[:].rearrange("c u p v -> c (u p v)").bitcast(F32)
+            turned = bank[:, : 2 * width].rearrange("p (m u c) -> p m u c", u=2, c=C)
+            for m, e in enumerate(group):
+                pairs = hs[e][:].rearrange("c u p v -> c (u p v)").bitcast(F32)
                 for u in range(2):
                     nc.tensor.transpose(turned[:, m, u, :], pairs[:, u * P : (u + 1) * P], identity[:])
             grouped = ring.tile([P, 4 * width], BF16, name="grouped", align_bytes=64)
             nc.scalar.copy(
                 out=grouped[:].bitcast(F32).rearrange("p (m c u) -> p m c u", c=C, u=2),
-                in_=turned[:].rearrange("p m u c -> p m c u"),
+                in_=turned.rearrange("p m u c -> p m c u"),
             )
-            h_word = ring.tile([P, width], U32, name="h_word", align_bytes=64)
-            h_plane = ring.tile([P, width], U8, name="h_plane", align_bytes=64)
+            h_word = held.tile([P, width], U32, name=f"h_word{group[0]}", align_bytes=64)
+            h_plane = held.tile([P, width], U8, name=f"h_plane{group[0]}", align_bytes=64)
             nc.vector.quantize_mx(out=h_word[:].bitcast(FP8X4), scales=h_plane[:], in_=grouped[:])
-            y_sum = psum.tile([P, width], F32, name="y_sum")
             for m, e in enumerate(group):
-                cols = slice(m * C, (m + 1) * C)
+                quantised[e] = (h_word[:, m * C : (m + 1) * C], h_plane[:, m * C : (m + 1) * C])
+
+        def second(experts, bank, copy):
+            for m, e in enumerate(experts):
+                h_word, h_plane = quantised[e]
                 nc.tensor.matmul_mx(
-                    out=y_sum[:, cols],
+                    out=bank[:, m * C : (m + 1) * C],
                     lhsT=w2[:, e, :].bitcast(FP4X4),
                     lhsT_scale=w2_plane[:, e, :],
-                    rhs=h_word[:, cols].bitcast(FP8X4),
-                    rhs_scale=h_plane[:, cols],
+                    rhs=h_word.bitcast(FP8X4),
+                    rhs_scale=h_plane,
                     start=True,
                     stop=True,
                 )
-            nc.scalar.copy(out=y[:, group[0] * C : group[0] * C + width], in_=y_sum[:])
+            copy(out=y[:, experts[0] * C : (experts[-1] + 1) * C], in_=bank[:, : len(experts) * C])
 
-        made = [hidden(e) for e in GROUPS[0]]
-        for before, group in zip(GROUPS, GROUPS[1:]):
-            ready = made
-            made = [hidden(e) for e in group]
-            second(before, ready)
-        second(GROUPS[-1], made)
+        hs, quantised = {}, {}
+        gather(0)
+        gather(1)
+        hidden(0)
+        hidden(1)
+        gather(2)
+        hidden(2)
+        hidden(3)
+        gather(3)
+        turn((0, 1), banks[1])
+        hidden(4)
+        turn((2, 3), banks[0])
+        hidden(5)
+        turn((4,), banks[1])
+        hidden(6)
+        hidden(7)
+        turn((5, 6), banks[1])
+        turn((7,), banks[2])
+        second((0, 1, 2, 3), banks[7], nc.vector.tensor_copy)
+        second((4, 5, 6), banks[0], nc.vector.tensor_copy)
+        second((7,), banks[3], nc.scalar.copy)
 
         for t0, t1 in CHUNKS:
             terms = []

@@ -41,8 +41,14 @@ def tile_moe_ecr_glu_gelu_kernel(tc, x_words, x_scales, w1_words, w1_scales, w3_
         ring = ctx.enter_context(tc.tile_pool(name="ring", bufs=2))
         psum = ctx.enter_context(tc.psum_pool(name="psum", bufs=1))
 
-        x_plane = held.tile([P, PASSES, T], U8, name="x_plane", align_bytes=64)
+        x_plane = held.tile([P, 2 * T], U8, name="x_plane", tag="tokens", align_bytes=64)
         nc.gpsimd.memset(x_plane[:].bitcast(I32), 0)
+        for q in range(4):
+            nc.scalar.dma_start(out=x_plane[32 * q : 32 * q + 8, :T].bitcast(I32), in_=x_scales[:, 4 * q : 4 * q + 4, :].bitcast(I32))
+        slot_plane = [held.tile([P, SLOTS], U8, name=f"slot_plane{s}", align_bytes=64) for s in range(PASSES)]
+        nc.gpsimd.memset(slot_plane[1][:].bitcast(I32), 0)
+        zeros = held.tile([P, PAD], F32, name="zeros")
+        nc.vector.memset(zeros[:], 0.0)
         w1_plane = [held.tile([P, HALF * PASSES, H], U8, name=f"w1_plane{g}", align_bytes=64) for g in range(2)]
         w3_plane = [held.tile([P, HALF * PASSES, H], U8, name=f"w3_plane{g}", align_bytes=64) for g in range(2)]
         w2_plane = held.tile([P, E, N], U8, name="w2_plane", align_bytes=64)
@@ -51,10 +57,8 @@ def tile_moe_ecr_glu_gelu_kernel(tc, x_words, x_scales, w1_words, w1_scales, w3_
 
         slot_list = held.tile([P, SLOTS // 16], U16, name="slot_list")
         nc.sync.dma_start(slot_list[:], offs)
-        x_word = [held.tile([P, T], U32, name=f"x_word{s}", align_bytes=64) for s in range(PASSES)]
-        nc.sync.dma_start(out=x_word[0][:].bitcast(I32), in_=x_words[0].rearrange("p t r -> p (t r)").bitcast(I32))
-        nc.sync.dma_start(out=x_word[1][:].bitcast(I32), in_=x_words[1].rearrange("p t r -> p (t r)").bitcast(I32))
-        load_scale_rows(nc, x_plane, x_scales)
+        x_word = held.tile([P, PASSES, T], U32, name="x_word", align_bytes=64)
+        nc.sync.dma_start(out=x_word[:].bitcast(I32), in_=x_words.rearrange("s p t r -> p s (t r)").bitcast(I32))
 
         w2 = held.tile([P, E, 2 * N], U8, name="w2", align_bytes=64)
         w1, w3 = {}, {}
@@ -67,6 +71,11 @@ def tile_moe_ecr_glu_gelu_kernel(tc, x_words, x_scales, w1_words, w1_scales, w3_
         def load_half(planes, scales, g):
             load_scale_rows(nc, planes[g], scales[g * HALF : (g + 1) * HALF].rearrange("e s q i -> (e s) q i"))
 
+        def gather_scales():
+            nc.vector.tensor_copy(slot_plane[0][:], x_plane[:].indirect(slot_list[:]))
+            for j in range(4):
+                nc.sync.dma_start(out=slot_plane[1][j:P:32, :].bitcast(I32), in_=slot_plane[0][4 + j : P : 32, :].bitcast(I32))
+
         for e in range(E):
             g, place = divmod(e, HALF)
             if place == 0:
@@ -77,6 +86,8 @@ def tile_moe_ecr_glu_gelu_kernel(tc, x_words, x_scales, w1_words, w1_scales, w3_
             if e == HALF:
                 load_scale_rows(nc, w2_plane, w2_scales.rearrange("e s q n -> (e s) q n"))
             w3[e] = load_words(w3_words, e, "w3")
+            if e == 0:
+                gather_scales()
         nc.sync.dma_start(out=w2[:].bitcast(I32), in_=w2_words.rearrange("e s p b -> p (e s) b").bitcast(I32))
 
         token_lists = []
@@ -91,29 +102,22 @@ def tile_moe_ecr_glu_gelu_kernel(tc, x_words, x_scales, w1_words, w1_scales, w3_
         identity = held.tile([P, P], F32, name="identity")
         make_identity(nc, identity[:])
         y = held.tile([P, SLOTS + PAD], F32, name="y")
-        nc.vector.memset(y[:, SLOTS:], 0.0)
+        nc.scalar.activation(out=y[:, SLOTS:], in_=zeros[:], func=GELU)
 
         banks = [psum.tile([P, H], F32, name=f"bank{b}") for b in range(8)]
-        slot_word, slot_plane = {}, {}
 
-        def gather(g):
-            offsets = slot_list[:, g * GATHER // 16 : (g + 1) * GATHER // 16]
-            slot_word[g], slot_plane[g] = [], []
+        slot_word = held.tile([P, PASSES * SLOTS], U32, name="slot_word", tag="tokens", align_bytes=64)
+        for c0 in range(0, SLOTS, GATHER):
             for s in range(PASSES):
-                words = ring.tile([P, GATHER], U32, name=f"slot_word{s}", align_bytes=64)
-                nc.vector.tensor_copy(words[:], x_word[s][:].indirect(offsets))
-                plane = ring.tile([P, GATHER], U8, name=f"slot_plane{s}", align_bytes=64, bufs=3)
-                nc.vector.tensor_copy(plane[:], x_plane[:, s, :].indirect(offsets))
-                slot_word[g].append(words)
-                slot_plane[g].append(plane)
+                nc.vector.tensor_copy(slot_word[:, s * SLOTS + c0 : s * SLOTS + c0 + GATHER], x_word[:, s, :].indirect(slot_list[:, c0 // 16 : (c0 + GATHER) // 16]))
 
         def first_product(e, words, plane, acc):
-            g, c0 = divmod(e * C, GATHER)
+            slots = slice(e * C, (e + 1) * C)
             for s in range(PASSES):
                 nc.tensor.matmul_mx(
                     out=acc[:],
-                    lhsT=slot_word[g][s][:, c0 : c0 + C].bitcast(FP8X4),
-                    lhsT_scale=slot_plane[g][s][:, c0 : c0 + C],
+                    lhsT=slot_word[:, s * SLOTS + e * C : s * SLOTS + (e + 1) * C].bitcast(FP8X4),
+                    lhsT_scale=slot_plane[s][:, slots],
                     rhs=words[:, s, :].bitcast(FP4X4),
                     rhs_scale=plane[e // HALF][:, e % HALF * PASSES + s, :],
                     start=(s == 0),
@@ -163,14 +167,10 @@ def tile_moe_ecr_glu_gelu_kernel(tc, x_words, x_scales, w1_words, w1_scales, w3_
             copy(out=y[:, experts[0] * C : (experts[-1] + 1) * C], in_=bank[:, : len(experts) * C])
 
         hs, quantised = {}, {}
-        gather(0)
-        gather(1)
         hidden(0)
         hidden(1)
-        gather(2)
         hidden(2)
         hidden(3)
-        gather(3)
         turn((0, 1), banks[1])
         hidden(4)
         turn((2, 3), banks[0])

@@ -28,10 +28,10 @@ HALF = E // 2
 CHUNKS = ((0, 512), (512, 768))
 
 
-def load_scale_rows(nc, plane, rows):
+def load_scale_rows(queue, plane, rows):
     by_j = rows.rearrange("g (q j) w -> j q g w", j=4)
     for j in range(4):
-        nc.sync.dma_start(out=plane[j:P:32, :, :].bitcast(I32), in_=by_j[j].bitcast(I32))
+        queue.dma_start(out=plane[j:P:32, :, :].bitcast(I32), in_=by_j[j].bitcast(I32))
 
 
 def tile_moe_ecr_glu_gelu_kernel(tc, x_words, x_scales, w1_words, w1_scales, w3_words, w3_scales, w2_words, w2_scales, gate, offs, pos1, pos2, pos3, out):
@@ -47,13 +47,13 @@ def tile_moe_ecr_glu_gelu_kernel(tc, x_words, x_scales, w1_words, w1_scales, w3_
             nc.scalar.dma_start(out=x_plane[32 * q : 32 * q + 8, :T].bitcast(I32), in_=x_scales[:, 4 * q : 4 * q + 4, :].bitcast(I32))
         slot_plane = [held.tile([P, SLOTS], U8, name=f"slot_plane{s}", align_bytes=64) for s in range(PASSES)]
         nc.gpsimd.memset(slot_plane[1][:].bitcast(I32), 0)
-        zeros = held.tile([P, PAD], F32, name="zeros")
-        nc.vector.memset(zeros[:], 0.0)
         w1_plane = [held.tile([P, HALF * PASSES, H], U8, name=f"w1_plane{g}", align_bytes=64) for g in range(2)]
         w3_plane = [held.tile([P, HALF * PASSES, H], U8, name=f"w3_plane{g}", align_bytes=64) for g in range(2)]
         w2_plane = held.tile([P, E, N], U8, name="w2_plane", align_bytes=64)
         for plane in (w1_plane[0], w3_plane[0], w1_plane[1], w3_plane[1], w2_plane):
             nc.vector.memset(plane[:].bitcast(I32), 0)
+        zeros = held.tile([P, PAD], F32, name="zeros")
+        nc.vector.memset(zeros[:], 0.0)
 
         slot_list = held.tile([P, SLOTS // 16], U16, name="slot_list")
         nc.sync.dma_start(slot_list[:], offs)
@@ -68,8 +68,8 @@ def tile_moe_ecr_glu_gelu_kernel(tc, x_words, x_scales, w1_words, w1_scales, w3_
             nc.sync.dma_start(out=tile[:].bitcast(I32), in_=words[e].rearrange("s p b -> p s b").bitcast(I32))
             return tile
 
-        def load_half(planes, scales, g):
-            load_scale_rows(nc, planes[g], scales[g * HALF : (g + 1) * HALF].rearrange("e s q i -> (e s) q i"))
+        def load_half(queue, planes, scales, g):
+            load_scale_rows(queue, planes[g], scales[g * HALF : (g + 1) * HALF].rearrange("e s q i -> (e s) q i"))
 
         def gather_scales():
             nc.vector.tensor_copy(slot_plane[0][:], x_plane[:].indirect(slot_list[:]))
@@ -77,17 +77,14 @@ def tile_moe_ecr_glu_gelu_kernel(tc, x_words, x_scales, w1_words, w1_scales, w3_
                 nc.sync.dma_start(out=slot_plane[1][j:P:32, :].bitcast(I32), in_=slot_plane[0][4 + j : P : 32, :].bitcast(I32))
 
         for e in range(E):
-            g, place = divmod(e, HALF)
-            if place == 0:
-                load_half(w1_plane, w1_scales, g)
-            w1[e] = load_words(w1_words, e, "w1")
-            if place == 0:
-                load_half(w3_plane, w3_scales, g)
-            if e == HALF:
-                load_scale_rows(nc, w2_plane, w2_scales.rearrange("e s q n -> (e s) q n"))
-            w3[e] = load_words(w3_words, e, "w3")
             if e == 0:
+                load_half(nc.sync, w1_plane, w1_scales, 0)
+            w1[e] = load_words(w1_words, e, "w1")
+            if e == 0:
+                load_half(nc.sync, w3_plane, w3_scales, 0)
                 gather_scales()
+            w3[e] = load_words(w3_words, e, "w3")
+        load_scale_rows(nc.sync, w2_plane, w2_scales.rearrange("e s q n -> (e s) q n"))
         nc.sync.dma_start(out=w2[:].bitcast(I32), in_=w2_words.rearrange("e s p b -> p (e s) b").bitcast(I32))
 
         token_lists = []
@@ -101,6 +98,8 @@ def tile_moe_ecr_glu_gelu_kernel(tc, x_words, x_scales, w1_words, w1_scales, w3_
 
         identity = held.tile([P, P], F32, name="identity")
         make_identity(nc, identity[:])
+        load_half(nc.gpsimd, w1_plane, w1_scales, 1)
+        load_half(nc.gpsimd, w3_plane, w3_scales, 1)
         y = held.tile([P, SLOTS + PAD], F32, name="y")
         nc.scalar.activation(out=y[:, SLOTS:], in_=zeros[:], func=GELU)
 
@@ -180,9 +179,9 @@ def tile_moe_ecr_glu_gelu_kernel(tc, x_words, x_scales, w1_words, w1_scales, w3_
         hidden(7)
         turn((5, 6), banks[1])
         turn((7,), banks[2])
-        second((0, 1, 2, 3), banks[7], nc.vector.tensor_copy)
+        second((0, 1, 2, 3), banks[3], nc.vector.tensor_copy)
         second((4, 5, 6), banks[0], nc.vector.tensor_copy)
-        second((7,), banks[3], nc.scalar.copy)
+        second((7,), banks[7], nc.scalar.copy)
 
         for t0, t1 in CHUNKS:
             terms = []

@@ -50,8 +50,9 @@ def tile_moe_ecr_glu_gelu_kernel(tc, x_words, x_scales, w1_words, w1_scales, w3_
         w1_plane = [held.tile([P, HALF * PASSES, H], U8, name=f"w1_plane{g}", align_bytes=64) for g in range(2)]
         w3_plane = [held.tile([P, HALF * PASSES, H], U8, name=f"w3_plane{g}", align_bytes=64) for g in range(2)]
         w2_plane = held.tile([P, E, N], U8, name="w2_plane", align_bytes=64)
-        for plane in (w1_plane[0], w3_plane[0], w1_plane[1], w3_plane[1], w2_plane):
+        for plane in (w1_plane[1], w1_plane[0], w3_plane[0], w3_plane[1]):
             nc.vector.memset(plane[:].bitcast(I32), 0)
+        nc.gpsimd.memset(w2_plane[:].bitcast(I32), 0)
         zeros = held.tile([P, PAD], F32, name="zeros")
         nc.vector.memset(zeros[:], 0.0)
 
@@ -64,9 +65,14 @@ def tile_moe_ecr_glu_gelu_kernel(tc, x_words, x_scales, w1_words, w1_scales, w3_
         w1, w3 = {}, {}
 
         def load_words(words, e, name):
+            if (name, e) == ("w3", E - 1):
+                tiles = [held.tile([P, 2 * H], U8, name=f"{name}_{e}_{s}", align_bytes=64) for s in range(PASSES)]
+                for s in range(PASSES):
+                    nc.sync.dma_start(out=tiles[s][:].bitcast(I32), in_=words[e, s].bitcast(I32))
+                return [tile[:] for tile in tiles]
             tile = held.tile([P, PASSES, 2 * H], U8, name=f"{name}_{e}", align_bytes=64)
             nc.sync.dma_start(out=tile[:].bitcast(I32), in_=words[e].rearrange("s p b -> p s b").bitcast(I32))
-            return tile
+            return [tile[:, s, :] for s in range(PASSES)]
 
         def load_half(queue, planes, scales, g):
             load_scale_rows(queue, planes[g], scales[g * HALF : (g + 1) * HALF].rearrange("e s q i -> (e s) q i"))
@@ -82,8 +88,9 @@ def tile_moe_ecr_glu_gelu_kernel(tc, x_words, x_scales, w1_words, w1_scales, w3_
             w1[e] = load_words(w1_words, e, "w1")
             if e == 0:
                 load_half(nc.sync, w3_plane, w3_scales, 0)
-                gather_scales()
             w3[e] = load_words(w3_words, e, "w3")
+            if e == 0:
+                gather_scales()
         load_scale_rows(nc.sync, w2_plane, w2_scales.rearrange("e s q n -> (e s) q n"))
         nc.sync.dma_start(out=w2[:].bitcast(I32), in_=w2_words.rearrange("e s p b -> p (e s) b").bitcast(I32))
 
@@ -117,7 +124,7 @@ def tile_moe_ecr_glu_gelu_kernel(tc, x_words, x_scales, w1_words, w1_scales, w3_
                     out=acc[:],
                     lhsT=slot_word[:, s * SLOTS + e * C : s * SLOTS + (e + 1) * C].bitcast(FP8X4),
                     lhsT_scale=slot_plane[s][:, slots],
-                    rhs=words[:, s, :].bitcast(FP4X4),
+                    rhs=words[s].bitcast(FP4X4),
                     rhs_scale=plane[e // HALF][:, e % HALF * PASSES + s, :],
                     start=(s == 0),
                     stop=(s == PASSES - 1),
@@ -129,17 +136,22 @@ def tile_moe_ecr_glu_gelu_kernel(tc, x_words, x_scales, w1_words, w1_scales, w3_
             b = first_product(e, w3[e], w3_plane, banks[2 + e % 5])
             act = ring.tile([P, 2, P, 2], F32, name="act", bufs=5)
             nc.scalar.activation(out=act[:], in_=a, func=GELU)
+            if e == E - 1:
+                hs[e] = [held.tile([P, P, 2], BF16, name=f"h_last{u}") for u in range(2)]
+                for u in range(2):
+                    nc.vector.tensor_tensor(out=hs[e][u][:], in0=b[:, u], in1=act[:, u], op=MULT)
+                hs[e] = [half[:] for half in hs[e]]
+                return
             h = ring.tile([P, 2, P, 2], BF16, name="h", bufs=8)
             nc.vector.tensor_tensor(out=h[:], in0=b, in1=act[:], op=MULT)
-            hs[e] = h
+            hs[e] = [h[:, u] for u in range(2)]
 
         def turn(group, bank):
             width = len(group) * C
             turned = bank[:, : 2 * width].rearrange("p (m u c) -> p m u c", u=2, c=C)
             for m, e in enumerate(group):
-                pairs = hs[e][:].rearrange("c u p v -> c (u p v)").bitcast(F32)
                 for u in range(2):
-                    nc.tensor.transpose(turned[:, m, u, :], pairs[:, u * P : (u + 1) * P], identity[:])
+                    nc.tensor.transpose(turned[:, m, u, :], hs[e][u].rearrange("c p v -> c (p v)").bitcast(F32), identity[:])
             grouped = ring.tile([P, 4 * width], BF16, name="grouped", align_bytes=64)
             nc.scalar.copy(
                 out=grouped[:].bitcast(F32).rearrange("p (m c u) -> p m c u", c=C, u=2),
@@ -174,24 +186,31 @@ def tile_moe_ecr_glu_gelu_kernel(tc, x_words, x_scales, w1_words, w1_scales, w3_
         hidden(4)
         turn((2, 3), banks[0])
         hidden(5)
-        turn((4,), banks[1])
         hidden(6)
+        turn((4, 5), banks[7])
         hidden(7)
-        turn((5, 6), banks[1])
-        turn((7,), banks[2])
-        second((0, 1, 2, 3), banks[3], nc.vector.tensor_copy)
-        second((4, 5, 6), banks[0], nc.vector.tensor_copy)
-        second((7,), banks[7], nc.scalar.copy)
+        second((0, 1, 2, 3), banks[2], nc.vector.tensor_copy)
+        turn((6,), banks[5])
+        turn((7,), banks[6])
+        second((4, 5, 6), banks[0], nc.scalar.copy)
+        second((7,), banks[1], nc.scalar.copy)
 
-        for t0, t1 in CHUNKS:
-            terms = []
-            for r in range(TOP):
+        terms = {}
+        for r in range(TOP):
+            for t0, t1 in CHUNKS:
                 term = held.tile([P, t1 - t0], F32, name=f"term{t0}_{r}")
                 nc.vector.tensor_tensor(term[:], y[:].indirect(token_lists[r][:, t0 // 16 : t1 // 16]), gates[r][:, t0:t1], MULT)
-                terms.append(term)
-                if r == 1:
-                    both = held.tile([P, t1 - t0], F32, name=f"both{t0}")
-                    nc.vector.tensor_tensor(both[:], terms[0][:], terms[1][:], ADD)
+                terms[r, t0] = term
+                if r < 2:
+                    for b in range(t0 // P, t1 // P):
+                        nc.tensor.matmul(banks[b][:, :N], lhsT=term[:, b * P - t0 : (b + 1) * P - t0], rhs=identity[:], is_transpose=True, start=(r == 0), stop=(r == 1))
+
+        for chunk, (t0, t1) in enumerate(CHUNKS):
+            back = banks[6 + chunk]
+            for b in range(t0 // P, t1 // P):
+                summed = held.tile([P, N], F32, name=f"summed{b}")
+                nc.scalar.copy(out=summed[:], in_=banks[b][:, :N])
+                nc.tensor.transpose(back[:, b * P - t0 : (b + 1) * P - t0], summed[:], identity[:])
             result = held.tile([P, t1 - t0], F32, name=f"result{t0}")
-            nc.vector.tensor_tensor(result[:], both[:], terms[2][:], ADD)
+            nc.vector.tensor_tensor(result[:], back[:, : t1 - t0], terms[2, t0][:], ADD)
             nc.sync.dma_start(out=out[:, t0:t1], in_=result[:])

@@ -25,6 +25,7 @@ GELU = mybir.ActivationFunctionType.Gelu_apprx_tanh
 
 GATHER = 256
 HALF = E // 2
+STEPS = ((0,), (1,), (2,), (3,), (4, 5), (6,), (7,))
 CHUNKS = ((0, 512), (512, 768))
 
 
@@ -42,7 +43,7 @@ def tile_moe_ecr_glu_gelu_kernel(tc, x_words, x_scales, w1_words, w1_scales, w3_
         psum = ctx.enter_context(tc.psum_pool(name="psum", bufs=1))
 
         x_plane = held.tile([P, 2 * T], U8, name="x_plane", tag="tokens", align_bytes=64)
-        nc.gpsimd.memset(x_plane[:].bitcast(I32), 0)
+        nc.vector.memset(x_plane[:].bitcast(I32), 0)
         for q in range(4):
             nc.scalar.dma_start(out=x_plane[32 * q : 32 * q + 8, :T].bitcast(I32), in_=x_scales[:, 4 * q : 4 * q + 4, :].bitcast(I32))
         slot_plane = [held.tile([P, SLOTS], U8, name=f"slot_plane{s}", align_bytes=64) for s in range(PASSES)]
@@ -82,26 +83,24 @@ def tile_moe_ecr_glu_gelu_kernel(tc, x_words, x_scales, w1_words, w1_scales, w3_
             for j in range(4):
                 nc.sync.dma_start(out=slot_plane[1][j:P:32, :].bitcast(I32), in_=slot_plane[0][4 + j : P : 32, :].bitcast(I32))
 
-        for e in range(E):
-            if e == 0:
-                load_half(nc.sync, w1_plane, w1_scales, 0)
-            w1[e] = load_words(w1_words, e, "w1")
-            if e == 0:
-                load_half(nc.sync, w3_plane, w3_scales, 0)
-            w3[e] = load_words(w3_words, e, "w3")
-            if e == 0:
-                gather_scales()
+        w1[0] = load_words(w1_words, 0, "w1")
+        load_half(nc.sync, w1_plane, w1_scales, 0)
+        load_half(nc.sync, w3_plane, w3_scales, 0)
+        w3[0] = load_words(w3_words, 0, "w3")
+        gather_scales()
+        for step in STEPS[1:]:
+            for e in step:
+                w1[e] = load_words(w1_words, e, "w1")
+            for e in step:
+                w3[e] = load_words(w3_words, e, "w3")
         load_scale_rows(nc.sync, w2_plane, w2_scales.rearrange("e s q n -> (e s) q n"))
         nc.sync.dma_start(out=w2[:].bitcast(I32), in_=w2_words.rearrange("e s p b -> p (e s) b").bitcast(I32))
 
-        token_lists = []
-        for r, pos in enumerate((pos1, pos2, pos3)):
-            token_list = held.tile([P, T // 16], U16, name=f"token_list{r}")
-            nc.sync.dma_start(token_list[:], pos)
-            token_lists.append(token_list)
         gates = [held.tile([P, T], F32, name=f"gate{r}") for r in range(TOP)]
-        for r in range(TOP):
+        token_lists = [held.tile([P, T // 16], U16, name=f"token_list{r}") for r in range(TOP)]
+        for r, pos in enumerate((pos1, pos2, pos3)):
             nc.sync.dma_start(out=gates[r][:], in_=gate[r])
+            nc.sync.dma_start(token_lists[r][:], pos)
 
         identity = held.tile([P, P], F32, name="identity")
         make_identity(nc, identity[:])
@@ -131,11 +130,14 @@ def tile_moe_ecr_glu_gelu_kernel(tc, x_words, x_scales, w1_words, w1_scales, w3_
                 )
             return acc[:].rearrange("c (p u v) -> c u p v", u=2, v=2)
 
-        def hidden(e):
+        def activate(e):
             a = first_product(e, w1[e], w1_plane, banks[e % 2])
-            b = first_product(e, w3[e], w3_plane, banks[2 + e % 5])
             act = ring.tile([P, 2, P, 2], F32, name="act", bufs=5)
             nc.scalar.activation(out=act[:], in_=a, func=GELU)
+            return act
+
+        def multiply(e, act):
+            b = first_product(e, w3[e], w3_plane, banks[2 + e % 5])
             if e == E - 1:
                 hs[e] = [held.tile([P, P, 2], BF16, name=f"h_last{u}") for u in range(2)]
                 for u in range(2):
@@ -146,14 +148,14 @@ def tile_moe_ecr_glu_gelu_kernel(tc, x_words, x_scales, w1_words, w1_scales, w3_
             nc.vector.tensor_tensor(out=h[:], in0=b, in1=act[:], op=MULT)
             hs[e] = [h[:, u] for u in range(2)]
 
-        def turn(group, bank):
+        def turn(group, bank, copy=nc.scalar.copy):
             width = len(group) * C
             turned = bank[:, : 2 * width].rearrange("p (m u c) -> p m u c", u=2, c=C)
             for m, e in enumerate(group):
                 for u in range(2):
                     nc.tensor.transpose(turned[:, m, u, :], hs[e][u].rearrange("c p v -> c (p v)").bitcast(F32), identity[:])
-            grouped = ring.tile([P, 4 * width], BF16, name="grouped", align_bytes=64)
-            nc.scalar.copy(
+            grouped = ring.tile([P, 4 * width], BF16, name="grouped", bufs=3, align_bytes=64)
+            copy(
                 out=grouped[:].bitcast(F32).rearrange("p (m c u) -> p m c u", c=C, u=2),
                 in_=turned.rearrange("p m u c -> p m c u"),
             )
@@ -178,22 +180,18 @@ def tile_moe_ecr_glu_gelu_kernel(tc, x_words, x_scales, w1_words, w1_scales, w3_
             copy(out=y[:, experts[0] * C : (experts[-1] + 1) * C], in_=bank[:, : len(experts) * C])
 
         hs, quantised = {}, {}
-        hidden(0)
-        hidden(1)
-        hidden(2)
-        hidden(3)
-        turn((0, 1), banks[1])
-        hidden(4)
-        turn((2, 3), banks[0])
-        hidden(5)
-        hidden(6)
-        turn((4, 5), banks[7])
-        hidden(7)
+        for step in STEPS:
+            acts = [activate(e) for e in step]
+            for e, act in zip(step, acts):
+                multiply(e, act)
+            if step[0] in (2, 4):
+                turn((step[0] - 2, step[0] - 1), banks[7])
+        turn((4, 5), banks[1], nc.vector.tensor_copy)
         second((0, 1, 2, 3), banks[2], nc.vector.tensor_copy)
         turn((6,), banks[5])
         turn((7,), banks[6])
         second((4, 5, 6), banks[0], nc.scalar.copy)
-        second((7,), banks[1], nc.scalar.copy)
+        second((7,), banks[7], nc.scalar.copy)
 
         terms = {}
         for r in range(TOP):

@@ -67,10 +67,10 @@ def tile_moe_ecr_glu_gelu_kernel(tc, x_words, x_scales, w1_words, w1_scales, w3_
 
         def load_words(words, e, name):
             if (name, e) == ("w3", E - 1):
-                tiles = [held.tile([P, 2 * H], U8, name=f"{name}_{e}_{s}", align_bytes=64) for s in range(PASSES)]
-                for s in range(PASSES):
-                    nc.sync.dma_start(out=tiles[s][:].bitcast(I32), in_=words[e, s].bitcast(I32))
-                return [tile[:] for tile in tiles]
+                halves = [held.tile([P, PASSES, H], U8, name=f"{name}_{e}_{m}", align_bytes=64) for m in range(2)]
+                for m in range(2):
+                    nc.sync.dma_start(out=halves[m][:].bitcast(I32), in_=words[e].rearrange("s p b -> p s b")[:, :, m * H : (m + 1) * H].bitcast(I32))
+                return halves
             tile = held.tile([P, PASSES, 2 * H], U8, name=f"{name}_{e}", align_bytes=64)
             nc.sync.dma_start(out=tile[:].bitcast(I32), in_=words[e].rearrange("s p b -> p s b").bitcast(I32))
             return [tile[:, s, :] for s in range(PASSES)]
@@ -87,10 +87,11 @@ def tile_moe_ecr_glu_gelu_kernel(tc, x_words, x_scales, w1_words, w1_scales, w3_
         load_half(nc.sync, w1_plane, w1_scales, 0)
         load_half(nc.sync, w3_plane, w3_scales, 0)
         w3[0] = load_words(w3_words, 0, "w3")
-        gather_scales()
         for step in STEPS[1:]:
             for e in step:
                 w1[e] = load_words(w1_words, e, "w1")
+            if step == STEPS[1]:
+                gather_scales()
             for e in step:
                 w3[e] = load_words(w3_words, e, "w3")
         load_scale_rows(nc.sync, w2_plane, w2_scales.rearrange("e s q n -> (e s) q n"))
@@ -136,14 +137,27 @@ def tile_moe_ecr_glu_gelu_kernel(tc, x_words, x_scales, w1_words, w1_scales, w3_
             nc.scalar.activation(out=act[:], in_=a, func=GELU)
             return act
 
+        def multiply_last(e, act):
+            h = held.tile([P, 2, P, 2], BF16, name="h_last")
+            for m, bank in enumerate((banks[4], banks[6])):
+                for c0 in range(0, H // 2, P):
+                    for s in range(PASSES):
+                        nc.tensor.matmul_mx(
+                            out=bank[:, c0 : c0 + P],
+                            lhsT=slot_word[:, s * SLOTS + e * C : s * SLOTS + (e + 1) * C].bitcast(FP8X4),
+                            lhsT_scale=slot_plane[s][:, e * C : (e + 1) * C],
+                            rhs=w3[e][m][:, s, 2 * c0 : 2 * (c0 + P)].bitcast(FP4X4),
+                            rhs_scale=w3_plane[1][:, e % HALF * PASSES + s, m * H // 2 + c0 : m * H // 2 + c0 + P],
+                            start=(s == 0),
+                            stop=(s == PASSES - 1),
+                        )
+                words = slice(m * P // 2, (m + 1) * P // 2)
+                b = bank[:, : H // 2].rearrange("c (p u v) -> c u p v", u=2, v=2)
+                nc.vector.tensor_tensor(out=h[:, :, words, :], in0=b, in1=act[:, :, words, :], op=MULT)
+            hs[e] = [h[:, u] for u in range(2)]
+
         def multiply(e, act):
             b = first_product(e, w3[e], w3_plane, banks[2 + e % 5])
-            if e == E - 1:
-                hs[e] = [held.tile([P, P, 2], BF16, name=f"h_last{u}") for u in range(2)]
-                for u in range(2):
-                    nc.vector.tensor_tensor(out=hs[e][u][:], in0=b[:, u], in1=act[:, u], op=MULT)
-                hs[e] = [half[:] for half in hs[e]]
-                return
             h = ring.tile([P, 2, P, 2], BF16, name="h", bufs=8)
             nc.vector.tensor_tensor(out=h[:], in0=b, in1=act[:], op=MULT)
             hs[e] = [h[:, u] for u in range(2)]
@@ -183,13 +197,13 @@ def tile_moe_ecr_glu_gelu_kernel(tc, x_words, x_scales, w1_words, w1_scales, w3_
         for step in STEPS:
             acts = [activate(e) for e in step]
             for e, act in zip(step, acts):
-                multiply(e, act)
+                (multiply if e < E - 1 else multiply_last)(e, act)
             if step[0] in (2, 4):
                 turn((step[0] - 2, step[0] - 1), banks[7])
         turn((4, 5), banks[1], nc.vector.tensor_copy)
         second((0, 1, 2, 3), banks[2], nc.vector.tensor_copy)
         turn((6,), banks[5])
-        turn((7,), banks[6])
+        turn((7,), banks[4])
         second((4, 5, 6), banks[0], nc.scalar.copy)
         second((7,), banks[7], nc.scalar.copy)
 

@@ -25,7 +25,7 @@ GELU = mybir.ActivationFunctionType.Gelu_apprx_tanh
 
 GATHER = 256
 HALF = E // 2
-STEPS = ((0,), (1,), (2,), (3,), (4, 5), (6,), (7,))
+STEPS = ((0,), (1,), (2,), (3,), (4, 5, 6), (7,))
 CHUNKS = ((0, 512), (512, 768))
 
 
@@ -200,11 +200,13 @@ def tile_moe_ecr_glu_gelu_kernel(tc, x_words, x_scales, w1_words, w1_scales, w3_
                 (multiply if e < E - 1 else multiply_last)(e, act)
             if step[0] in (2, 4):
                 turn((step[0] - 2, step[0] - 1), banks[7])
-        turn((4, 5), banks[1], nc.vector.tensor_copy)
-        second((0, 1, 2, 3), banks[2], nc.vector.tensor_copy)
+            if step[0] == 4:
+                turn((4,), banks[7])
+        turn((5,), banks[1], nc.vector.tensor_copy)
         turn((6,), banks[5])
         turn((7,), banks[4])
-        second((4, 5, 6), banks[0], nc.scalar.copy)
+        second((0, 1, 2, 3), banks[2], nc.scalar.copy)
+        second((4, 5, 6), banks[0], nc.vector.tensor_copy)
         second((7,), banks[7], nc.scalar.copy)
 
         terms = {}

@@ -27,6 +27,7 @@ GATHER = 256
 HALF = E // 2
 STEPS = ((0,), (1,), (2,), (3,), (4, 5, 6), (7,))
 CHUNKS = ((0, 512), (512, 768))
+STORE = 256
 
 
 def load_scale_rows(queue, plane, rows):
@@ -97,11 +98,13 @@ def tile_moe_ecr_glu_gelu_kernel(tc, x_words, x_scales, w1_words, w1_scales, w3_
         load_scale_rows(nc.sync, w2_plane, w2_scales.rearrange("e s q n -> (e s) q n"))
         nc.sync.dma_start(out=w2[:].bitcast(I32), in_=w2_words.rearrange("e s p b -> p (e s) b").bitcast(I32))
 
-        gates = [held.tile([P, T], F32, name=f"gate{r}") for r in range(TOP)]
+        gates = {(r, t0): held.tile([P, t1 - t0], F32, name=f"gate{r}_{t0}") for r in range(TOP) for t0, t1 in CHUNKS}
         token_lists = [held.tile([P, T // 16], U16, name=f"token_list{r}") for r in range(TOP)]
-        for r, pos in enumerate((pos1, pos2, pos3)):
-            nc.sync.dma_start(out=gates[r][:], in_=gate[r])
-            nc.sync.dma_start(token_lists[r][:], pos)
+        combine = [(r, chunk) for chunk in CHUNKS for r in range(2)] + [(2, chunk) for chunk in CHUNKS]
+        for r, (t0, t1) in combine:
+            nc.sync.dma_start(out=gates[r, t0][:], in_=gate[TOP - 1 - r][:, t0:t1])
+            if t0 == 0:
+                nc.sync.dma_start(token_lists[r][:], (pos3, pos2, pos1)[r])
 
         identity = held.tile([P, P], F32, name="identity")
         make_identity(nc, identity[:])
@@ -210,14 +213,13 @@ def tile_moe_ecr_glu_gelu_kernel(tc, x_words, x_scales, w1_words, w1_scales, w3_
         second((7,), banks[7], nc.scalar.copy)
 
         terms = {}
-        for r in range(TOP):
-            for t0, t1 in CHUNKS:
-                term = held.tile([P, t1 - t0], F32, name=f"term{t0}_{r}")
-                nc.vector.tensor_tensor(term[:], y[:].indirect(token_lists[r][:, t0 // 16 : t1 // 16]), gates[r][:, t0:t1], MULT)
-                terms[r, t0] = term
-                if r < 2:
-                    for b in range(t0 // P, t1 // P):
-                        nc.tensor.matmul(banks[b][:, :N], lhsT=term[:, b * P - t0 : (b + 1) * P - t0], rhs=identity[:], is_transpose=True, start=(r == 0), stop=(r == 1))
+        for r, (t0, t1) in combine:
+            term = held.tile([P, t1 - t0], F32, name=f"term{t0}_{r}")
+            nc.vector.tensor_tensor(term[:], y[:].indirect(token_lists[r][:, t0 // 16 : t1 // 16]), gates[r, t0][:], MULT)
+            terms[r, t0] = term
+            if r < 2:
+                for b in range(t0 // P, t1 // P):
+                    nc.tensor.matmul(banks[b][:, :N], lhsT=term[:, b * P - t0 : (b + 1) * P - t0], rhs=identity[:], is_transpose=True, start=(r == 0), stop=(r == 1))
 
         for chunk, (t0, t1) in enumerate(CHUNKS):
             back = banks[6 + chunk]
@@ -225,6 +227,7 @@ def tile_moe_ecr_glu_gelu_kernel(tc, x_words, x_scales, w1_words, w1_scales, w3_
                 summed = held.tile([P, N], F32, name=f"summed{b}")
                 nc.scalar.copy(out=summed[:], in_=banks[b][:, :N])
                 nc.tensor.transpose(back[:, b * P - t0 : (b + 1) * P - t0], summed[:], identity[:])
-            result = held.tile([P, t1 - t0], F32, name=f"result{t0}")
-            nc.vector.tensor_tensor(result[:], back[:, : t1 - t0], terms[2, t0][:], ADD)
-            nc.sync.dma_start(out=out[:, t0:t1], in_=result[:])
+            for c0 in range(0, t1 - t0, STORE):
+                result = held.tile([P, STORE], F32, name=f"result{t0 + c0}")
+                nc.vector.tensor_tensor(result[:], back[:, c0 : c0 + STORE], terms[2, t0][:, c0 : c0 + STORE], ADD)
+                nc.sync.dma_start(out=out[:, t0 + c0 : t0 + c0 + STORE], in_=result[:])

@@ -26,8 +26,9 @@ GELU = mybir.ActivationFunctionType.Gelu_apprx_tanh
 GATHER = 256
 HALF = E // 2
 STEPS = ((0,), (1,), (2,), (3,), (4, 5, 6), (7,))
-CHUNKS = ((0, 512), (512, 768))
-STORE = 256
+CHUNK = 256
+BLOCKS = T // P
+COPY = mybir.ActivationFunctionType.Copy
 
 
 def load_scale_rows(queue, plane, rows):
@@ -95,16 +96,18 @@ def tile_moe_ecr_glu_gelu_kernel(tc, x_words, x_scales, w1_words, w1_scales, w3_
                 gather_scales()
             for e in step:
                 w3[e] = load_words(w3_words, e, "w3")
+        gate_rows = held.tile([P, P], F32, name="gate_rows")
+        nc.sync.dma_start(out=gate_rows[:], in_=gate[0].rearrange("n (b t) -> (n b) t", t=P)[:P])
         load_scale_rows(nc.sync, w2_plane, w2_scales.rearrange("e s q n -> (e s) q n"))
         nc.sync.dma_start(out=w2[:].bitcast(I32), in_=w2_words.rearrange("e s p b -> p (e s) b").bitcast(I32))
 
-        gates = {(r, t0): held.tile([P, t1 - t0], F32, name=f"gate{r}_{t0}") for r in range(TOP) for t0, t1 in CHUNKS}
         token_lists = [held.tile([P, T // 16], U16, name=f"token_list{r}") for r in range(TOP)]
-        combine = [(r, chunk) for chunk in CHUNKS for r in range(2)] + [(2, chunk) for chunk in CHUNKS]
-        for r, (t0, t1) in combine:
-            nc.sync.dma_start(out=gates[r, t0][:], in_=gate[TOP - 1 - r][:, t0:t1])
-            if t0 == 0:
-                nc.sync.dma_start(token_lists[r][:], (pos3, pos2, pos1)[r])
+        gates = {r: held.tile([P, T], F32, name=f"gate{r}") for r in (1, 2)}
+        nc.sync.dma_start(token_lists[0][:], pos1)
+        nc.sync.dma_start(token_lists[2][:], pos3)
+        nc.sync.dma_start(out=gates[2][:], in_=gate[2])
+        nc.sync.dma_start(token_lists[1][:], pos2)
+        nc.sync.dma_start(out=gates[1][:], in_=gate[1])
 
         identity = held.tile([P, P], F32, name="identity")
         make_identity(nc, identity[:])
@@ -208,26 +211,56 @@ def tile_moe_ecr_glu_gelu_kernel(tc, x_words, x_scales, w1_words, w1_scales, w3_
         turn((5,), banks[1], nc.vector.tensor_copy)
         turn((6,), banks[5])
         turn((7,), banks[4])
+        gate_column = held.tile([P, BLOCKS], F32, name="gate_column")
+        nc.tensor.transpose(banks[3][:, :P], gate_rows[:], identity[:])
+        nc.scalar.copy(out=gate_column[:], in_=banks[3][:, :BLOCKS])
         second((0, 1, 2, 3), banks[2], nc.scalar.copy)
         second((4, 5, 6), banks[0], nc.vector.tensor_copy)
         second((7,), banks[7], nc.scalar.copy)
 
-        terms = {}
-        for r, (t0, t1) in combine:
-            term = held.tile([P, t1 - t0], F32, name=f"term{t0}_{r}")
-            nc.vector.tensor_tensor(term[:], y[:].indirect(token_lists[r][:, t0 // 16 : t1 // 16]), gates[r, t0][:], MULT)
-            terms[r, t0] = term
-            if r < 2:
-                for b in range(t0 // P, t1 // P):
-                    nc.tensor.matmul(banks[b][:, :N], lhsT=term[:, b * P - t0 : (b + 1) * P - t0], rhs=identity[:], is_transpose=True, start=(r == 0), stop=(r == 1))
+        def picked(r, t0, t1):
+            return y[:].indirect(token_lists[r][:, t0 // 16 : t1 // 16])
 
-        for chunk, (t0, t1) in enumerate(CHUNKS):
-            back = banks[6 + chunk]
-            for b in range(t0 // P, t1 // P):
-                summed = held.tile([P, N], F32, name=f"summed{b}")
-                nc.scalar.copy(out=summed[:], in_=banks[b][:, :N])
-                nc.tensor.transpose(back[:, b * P - t0 : (b + 1) * P - t0], summed[:], identity[:])
-            for c0 in range(0, t1 - t0, STORE):
-                result = held.tile([P, STORE], F32, name=f"result{t0 + c0}")
-                nc.vector.tensor_tensor(result[:], back[:, c0 : c0 + STORE], terms[2, t0][:, c0 : c0 + STORE], ADD)
-                nc.sync.dma_start(out=out[:, t0 + c0 : t0 + c0 + STORE], in_=result[:])
+        def gated(r, t0, t1):
+            term = held.tile([P, t1 - t0], F32, name=f"term{r}_{t0}")
+            nc.vector.tensor_tensor(term[:], picked(r, t0, t1), gates[r][:, t0:t1], MULT)
+            return term
+
+        def fetch(c):
+            t0 = c * CHUNK
+            plain = held.tile([P, CHUNK], F32, name=f"plain{c}")
+            nc.scalar.activation(out=plain[:], in_=picked(0, t0, t0 + CHUNK), func=COPY)
+            for b0 in range(0, CHUNK, P):
+                nc.tensor.transpose(banks[1 + c][:, b0 : b0 + P], plain[:, b0 : b0 + P], identity[:])
+
+        def weigh(c, extra=None):
+            t0 = c * CHUNK
+            parts = [held.tile([P, CHUNK], F32, name=f"by_token{c}")]
+            for b0 in range(0, CHUNK, P):
+                b = (t0 + b0) // P
+                nc.scalar.activation(out=parts[0][:, b0 : b0 + P], in_=banks[1 + c][:, b0 : b0 + P], func=COPY, scale=gate_column[:, b : b + 1])
+            if extra is not None:
+                parts.append(held.tile([P, CHUNK], F32, name="extra_by_token"))
+                nc.scalar.copy(out=parts[1][:], in_=extra)
+            for b0 in range(0, CHUNK, P):
+                for n, part in enumerate(parts):
+                    nc.tensor.matmul(banks[4 + c][:, b0 : b0 + P], lhsT=part[:, b0 : b0 + P], rhs=identity[:], is_transpose=True, start=(n == 0), stop=(n == len(parts) - 1))
+
+        fetch(0)
+        first3 = gated(2, 0, CHUNK)
+        for b0 in range(0, CHUNK, P):
+            nc.tensor.transpose(banks[0][:, b0 : b0 + P], first3[:, b0 : b0 + P], identity[:])
+        fetch(1)
+        weigh(0, banks[0][:, :CHUNK])
+        fetch(2)
+        weigh(1)
+        weigh(2)
+        rest3 = gated(2, CHUNK, T)
+        rest2 = gated(1, CHUNK, T)
+        first2 = gated(1, 0, CHUNK)
+        rest = held.tile([P, T - CHUNK], F32, name="rest")
+        nc.vector.tensor_tensor(rest[:], rest3[:], rest2[:], ADD)
+        for c, term in enumerate((first2[:], rest[:, :CHUNK], rest[:, CHUNK:])):
+            result = held.tile([P, CHUNK], F32, name=f"result{c}")
+            nc.vector.tensor_tensor(result[:], banks[4 + c][:, :CHUNK], term, ADD)
+            nc.sync.dma_start(out=out[:, c * CHUNK : (c + 1) * CHUNK], in_=result[:])

@@ -28,6 +28,8 @@ HALF = E // 2
 STEPS = ((0,), (1,), (2,), (3,), (4, 5, 6), (7,))
 CHUNK = 256
 BLOCKS = T // P
+GATE_STEP = 17
+GATE_ROW = {divmod(k * GATE_STEP, N * BLOCKS)[0] * BLOCKS + k * GATE_STEP % BLOCKS: k for k in range(P)}
 COPY = mybir.ActivationFunctionType.Copy
 
 
@@ -59,6 +61,8 @@ def tile_moe_ecr_glu_gelu_kernel(tc, x_words, x_scales, w1_words, w1_scales, w3_
         zeros = held.tile([P, PAD], F32, name="zeros")
         nc.vector.memset(zeros[:], 0.0)
 
+        gate_rows = held.tile([P, P], F32, name="gate_rows")
+        nc.scalar.dma_start(out=gate_rows[:], in_=gate.rearrange("r n (b t) -> (r n b) t", t=P)[0 : P * GATE_STEP : GATE_STEP])
         slot_list = held.tile([P, SLOTS // 16], U16, name="slot_list")
         nc.sync.dma_start(slot_list[:], offs)
         x_word = held.tile([P, PASSES, T], U32, name="x_word", align_bytes=64)
@@ -96,18 +100,12 @@ def tile_moe_ecr_glu_gelu_kernel(tc, x_words, x_scales, w1_words, w1_scales, w3_
                 gather_scales()
             for e in step:
                 w3[e] = load_words(w3_words, e, "w3")
-        gate_rows = held.tile([P, P], F32, name="gate_rows")
-        nc.sync.dma_start(out=gate_rows[:], in_=gate[0].rearrange("n (b t) -> (n b) t", t=P)[:P])
         load_scale_rows(nc.sync, w2_plane, w2_scales.rearrange("e s q n -> (e s) q n"))
         nc.sync.dma_start(out=w2[:].bitcast(I32), in_=w2_words.rearrange("e s p b -> p (e s) b").bitcast(I32))
 
         token_lists = [held.tile([P, T // 16], U16, name=f"token_list{r}") for r in range(TOP)]
-        gates = {r: held.tile([P, T], F32, name=f"gate{r}") for r in (1, 2)}
-        nc.sync.dma_start(token_lists[0][:], pos1)
-        nc.sync.dma_start(token_lists[2][:], pos3)
-        nc.sync.dma_start(out=gates[2][:], in_=gate[2])
-        nc.sync.dma_start(token_lists[1][:], pos2)
-        nc.sync.dma_start(out=gates[1][:], in_=gate[1])
+        for r, pos in ((0, pos1), (2, pos3), (1, pos2)):
+            nc.sync.dma_start(token_lists[r][:], pos)
 
         identity = held.tile([P, P], F32, name="identity")
         make_identity(nc, identity[:])
@@ -117,6 +115,17 @@ def tile_moe_ecr_glu_gelu_kernel(tc, x_words, x_scales, w1_words, w1_scales, w3_
         nc.scalar.activation(out=y[:, SLOTS:], in_=zeros[:], func=GELU)
 
         banks = [psum.tile([P, H], F32, name=f"bank{b}") for b in range(8)]
+
+        gate_column = held.tile([P, P], F32, name="gate_column")
+        nc.tensor.transpose(banks[4][:, :P], gate_rows[:], identity[:])
+        nc.scalar.copy(out=gate_column[:], in_=banks[4][:, :P])
+        spread = held.tile([P, 2 * T], F32, name="spread")
+        for m in range(2 * BLOCKS):
+            k = GATE_ROW[BLOCKS + m]
+            nc.tensor.transpose(banks[5 + m // 4][:, m % 4 * P : (m % 4 + 1) * P], gate_column[:, k : k + 1].to_broadcast([P, P]), identity[:])
+            if m % 4 == 3:
+                nc.scalar.copy(out=spread[:, (m - 3) * P : (m + 1) * P], in_=banks[5 + m // 4][:])
+        gates = {r: spread[:, (r - 1) * T : r * T] for r in (1, 2)}
 
         slot_word = held.tile([P, PASSES * SLOTS], U32, name="slot_word", tag="tokens", align_bytes=64)
         for c0 in range(0, SLOTS, GATHER):
@@ -211,9 +220,6 @@ def tile_moe_ecr_glu_gelu_kernel(tc, x_words, x_scales, w1_words, w1_scales, w3_
         turn((5,), banks[1], nc.vector.tensor_copy)
         turn((6,), banks[5])
         turn((7,), banks[4])
-        gate_column = held.tile([P, BLOCKS], F32, name="gate_column")
-        nc.tensor.transpose(banks[3][:, :P], gate_rows[:], identity[:])
-        nc.scalar.copy(out=gate_column[:], in_=banks[3][:, :BLOCKS])
         second((0, 1, 2, 3), banks[2], nc.scalar.copy)
         second((4, 5, 6), banks[0], nc.vector.tensor_copy)
         second((7,), banks[7], nc.scalar.copy)
@@ -237,7 +243,7 @@ def tile_moe_ecr_glu_gelu_kernel(tc, x_words, x_scales, w1_words, w1_scales, w3_
             t0 = c * CHUNK
             parts = [held.tile([P, CHUNK], F32, name=f"by_token{c}")]
             for b0 in range(0, CHUNK, P):
-                b = (t0 + b0) // P
+                b = GATE_ROW[(t0 + b0) // P]
                 nc.scalar.activation(out=parts[0][:, b0 : b0 + P], in_=banks[1 + c][:, b0 : b0 + P], func=COPY, scale=gate_column[:, b : b + 1])
             if extra is not None:
                 parts.append(held.tile([P, CHUNK], F32, name="extra_by_token"))

@@ -104,7 +104,7 @@ def tile_moe_ecr_glu_gelu_kernel(tc, x_words, x_scales, w1_words, w1_scales, w3_
         nc.sync.dma_start(out=w2[:].bitcast(I32), in_=w2_words.rearrange("e s p b -> p (e s) b").bitcast(I32))
 
         token_lists = [held.tile([P, T // 16], U16, name=f"token_list{r}") for r in range(TOP)]
-        for r, pos in ((0, pos1), (2, pos3), (1, pos2)):
+        for r, pos in ((2, pos3), (1, pos2), (0, pos1)):
             nc.sync.dma_start(token_lists[r][:], pos)
 
         identity = held.tile([P, P], F32, name="identity")
@@ -121,11 +121,11 @@ def tile_moe_ecr_glu_gelu_kernel(tc, x_words, x_scales, w1_words, w1_scales, w3_
         nc.scalar.copy(out=gate_column[:], in_=banks[4][:, :P])
         spread = held.tile([P, 2 * T], F32, name="spread")
         for m in range(2 * BLOCKS):
-            k = GATE_ROW[BLOCKS + m]
+            k = GATE_ROW[m]
             nc.tensor.transpose(banks[5 + m // 4][:, m % 4 * P : (m % 4 + 1) * P], gate_column[:, k : k + 1].to_broadcast([P, P]), identity[:])
             if m % 4 == 3:
                 nc.scalar.copy(out=spread[:, (m - 3) * P : (m + 1) * P], in_=banks[5 + m // 4][:])
-        gates = {r: spread[:, (r - 1) * T : r * T] for r in (1, 2)}
+        gates = [spread[:, r * T : (r + 1) * T] for r in range(2)]
 
         slot_word = held.tile([P, PASSES * SLOTS], U32, name="slot_word", tag="tokens", align_bytes=64)
         for c0 in range(0, SLOTS, GATHER):
@@ -235,7 +235,7 @@ def tile_moe_ecr_glu_gelu_kernel(tc, x_words, x_scales, w1_words, w1_scales, w3_
         def fetch(c):
             t0 = c * CHUNK
             plain = held.tile([P, CHUNK], F32, name=f"plain{c}")
-            nc.scalar.activation(out=plain[:], in_=picked(0, t0, t0 + CHUNK), func=COPY)
+            nc.scalar.activation(out=plain[:], in_=picked(2, t0, t0 + CHUNK), func=COPY)
             for b0 in range(0, CHUNK, P):
                 nc.tensor.transpose(banks[1 + c][:, b0 : b0 + P], plain[:, b0 : b0 + P], identity[:])
 
@@ -243,7 +243,7 @@ def tile_moe_ecr_glu_gelu_kernel(tc, x_words, x_scales, w1_words, w1_scales, w3_
             t0 = c * CHUNK
             parts = [held.tile([P, CHUNK], F32, name=f"by_token{c}")]
             for b0 in range(0, CHUNK, P):
-                b = GATE_ROW[(t0 + b0) // P]
+                b = GATE_ROW[2 * BLOCKS + (t0 + b0) // P]
                 nc.scalar.activation(out=parts[0][:, b0 : b0 + P], in_=banks[1 + c][:, b0 : b0 + P], func=COPY, scale=gate_column[:, b : b + 1])
             if extra is not None:
                 parts.append(held.tile([P, CHUNK], F32, name="extra_by_token"))
@@ -253,20 +253,20 @@ def tile_moe_ecr_glu_gelu_kernel(tc, x_words, x_scales, w1_words, w1_scales, w3_
                     nc.tensor.matmul(banks[4 + c][:, b0 : b0 + P], lhsT=part[:, b0 : b0 + P], rhs=identity[:], is_transpose=True, start=(n == 0), stop=(n == len(parts) - 1))
 
         fetch(0)
-        first3 = gated(2, 0, CHUNK)
+        first2 = gated(1, 0, CHUNK)
         for b0 in range(0, CHUNK, P):
-            nc.tensor.transpose(banks[0][:, b0 : b0 + P], first3[:, b0 : b0 + P], identity[:])
+            nc.tensor.transpose(banks[0][:, b0 : b0 + P], first2[:, b0 : b0 + P], identity[:])
         fetch(1)
-        weigh(0, banks[0][:, :CHUNK])
         fetch(2)
+        weigh(0, banks[0][:, :CHUNK])
         weigh(1)
         weigh(2)
-        rest3 = gated(2, CHUNK, T)
         rest2 = gated(1, CHUNK, T)
-        first2 = gated(1, 0, CHUNK)
+        rest1 = gated(0, CHUNK, T)
+        first1 = gated(0, 0, CHUNK)
         rest = held.tile([P, T - CHUNK], F32, name="rest")
-        nc.vector.tensor_tensor(rest[:], rest3[:], rest2[:], ADD)
-        for c, term in enumerate((first2[:], rest[:, :CHUNK], rest[:, CHUNK:])):
+        nc.vector.tensor_tensor(rest[:], rest2[:], rest1[:], ADD)
+        for c, term in enumerate((first1[:], rest[:, :CHUNK], rest[:, CHUNK:])):
             result = held.tile([P, CHUNK], F32, name=f"result{c}")
             nc.vector.tensor_tensor(result[:], banks[4 + c][:, :CHUNK], term, ADD)
             nc.sync.dma_start(out=out[:, c * CHUNK : (c + 1) * CHUNK], in_=result[:])

@@ -26,10 +26,9 @@ GELU = mybir.ActivationFunctionType.Gelu_apprx_tanh
 GATHER = 256
 HALF = E // 2
 STEPS = ((0,), (1,), (2,), (3,), (4, 5, 6), (7,))
-CHUNK = 256
+CHUNKS = ((0, 256), (256, 512), (512, 768))
+TURNED = 1
 BLOCKS = T // P
-GATE_STEP = 17
-GATE_ROW = {divmod(k * GATE_STEP, N * BLOCKS)[0] * BLOCKS + k * GATE_STEP % BLOCKS: k for k in range(P)}
 COPY = mybir.ActivationFunctionType.Copy
 
 
@@ -48,8 +47,9 @@ def tile_moe_ecr_glu_gelu_kernel(tc, x_words, x_scales, w1_words, w1_scales, w3_
 
         x_plane = held.tile([P, 2 * T], U8, name="x_plane", tag="tokens", align_bytes=64)
         nc.vector.memset(x_plane[:].bitcast(I32), 0)
-        for q in range(4):
-            nc.scalar.dma_start(out=x_plane[32 * q : 32 * q + 8, :T].bitcast(I32), in_=x_scales[:, 4 * q : 4 * q + 4, :].bitcast(I32))
+        x_rows = x_scales.rearrange("s (q j) t -> j q s t", j=4)
+        for j in range(4):
+            nc.scalar.dma_start(out=x_plane[j:P:16, :T].bitcast(I32), in_=x_rows[j].bitcast(I32))
         slot_plane = [held.tile([P, SLOTS], U8, name=f"slot_plane{s}", align_bytes=64) for s in range(PASSES)]
         nc.gpsimd.memset(slot_plane[1][:].bitcast(I32), 0)
         w1_plane = [held.tile([P, HALF * PASSES, H], U8, name=f"w1_plane{g}", align_bytes=64) for g in range(2)]
@@ -61,14 +61,12 @@ def tile_moe_ecr_glu_gelu_kernel(tc, x_words, x_scales, w1_words, w1_scales, w3_
         zeros = held.tile([P, PAD], F32, name="zeros")
         nc.vector.memset(zeros[:], 0.0)
 
-        gate_rows = held.tile([P, P], F32, name="gate_rows")
-        nc.scalar.dma_start(out=gate_rows[:], in_=gate.rearrange("r n (b t) -> (r n b) t", t=P)[0 : P * GATE_STEP : GATE_STEP])
         slot_list = held.tile([P, SLOTS // 16], U16, name="slot_list")
         nc.sync.dma_start(slot_list[:], offs)
         x_word = held.tile([P, PASSES, T], U32, name="x_word", align_bytes=64)
         nc.sync.dma_start(out=x_word[:].bitcast(I32), in_=x_words.rearrange("s p t r -> p s (t r)").bitcast(I32))
 
-        w2 = held.tile([P, E, 2 * N], U8, name="w2", align_bytes=64)
+        w2 = [held.tile([P, HALF, 2 * N], U8, name=f"w2_{g}", align_bytes=64) for g in range(2)]
         w1, w3 = {}, {}
 
         def load_words(words, e, name):
@@ -87,7 +85,7 @@ def tile_moe_ecr_glu_gelu_kernel(tc, x_words, x_scales, w1_words, w1_scales, w3_
         def gather_scales():
             nc.vector.tensor_copy(slot_plane[0][:], x_plane[:].indirect(slot_list[:]))
             for j in range(4):
-                nc.sync.dma_start(out=slot_plane[1][j:P:32, :].bitcast(I32), in_=slot_plane[0][4 + j : P : 32, :].bitcast(I32))
+                nc.sync.dma_start(out=slot_plane[1][j:P:32, :].bitcast(I32), in_=slot_plane[0][16 + j : P : 32, :].bitcast(I32))
 
         w1[0] = load_words(w1_words, 0, "w1")
         load_half(nc.sync, w1_plane, w1_scales, 0)
@@ -100,12 +98,27 @@ def tile_moe_ecr_glu_gelu_kernel(tc, x_words, x_scales, w1_words, w1_scales, w3_
                 gather_scales()
             for e in step:
                 w3[e] = load_words(w3_words, e, "w3")
+        gate_rows = held.tile([P, P], F32, name="gate_rows")
+        nc.sync.dma_start(out=gate_rows[:], in_=gate[2].rearrange("n (b t) -> (n b) t", t=P)[:P])
         load_scale_rows(nc.sync, w2_plane, w2_scales.rearrange("e s q n -> (e s) q n"))
-        nc.sync.dma_start(out=w2[:].bitcast(I32), in_=w2_words.rearrange("e s p b -> p (e s) b").bitcast(I32))
+        for g in range(2):
+            nc.sync.dma_start(out=w2[g][:].bitcast(I32), in_=w2_words[g * HALF : (g + 1) * HALF].rearrange("e s p b -> p (e s) b").bitcast(I32))
 
         token_lists = [held.tile([P, T // 16], U16, name=f"token_list{r}") for r in range(TOP)]
-        for r, pos in ((2, pos3), (1, pos2), (0, pos1)):
-            nc.sync.dma_start(token_lists[r][:], pos)
+        split = CHUNKS[TURNED][0]
+        gates = {}
+
+        def load_gate(r, t0, t1):
+            gates[r, t0] = held.tile([P, t1 - t0], F32, name=f"gate{r}_{t0}")
+            nc.sync.dma_start(out=gates[r, t0][:], in_=gate[r][:, t0:t1])
+
+        nc.sync.dma_start(token_lists[2][:], pos3)
+        nc.sync.dma_start(token_lists[1][:], pos2)
+        load_gate(1, 0, split)
+        load_gate(1, split, T)
+        nc.sync.dma_start(token_lists[0][:], pos1)
+        load_gate(0, split, T)
+        load_gate(0, 0, split)
 
         identity = held.tile([P, P], F32, name="identity")
         make_identity(nc, identity[:])
@@ -115,17 +128,6 @@ def tile_moe_ecr_glu_gelu_kernel(tc, x_words, x_scales, w1_words, w1_scales, w3_
         nc.scalar.activation(out=y[:, SLOTS:], in_=zeros[:], func=GELU)
 
         banks = [psum.tile([P, H], F32, name=f"bank{b}") for b in range(8)]
-
-        gate_column = held.tile([P, P], F32, name="gate_column")
-        nc.tensor.transpose(banks[4][:, :P], gate_rows[:], identity[:])
-        nc.scalar.copy(out=gate_column[:], in_=banks[4][:, :P])
-        spread = held.tile([P, 2 * T], F32, name="spread")
-        for m in range(2 * BLOCKS):
-            k = GATE_ROW[m]
-            nc.tensor.transpose(banks[5 + m // 4][:, m % 4 * P : (m % 4 + 1) * P], gate_column[:, k : k + 1].to_broadcast([P, P]), identity[:])
-            if m % 4 == 3:
-                nc.scalar.copy(out=spread[:, (m - 3) * P : (m + 1) * P], in_=banks[5 + m // 4][:])
-        gates = [spread[:, r * T : (r + 1) * T] for r in range(2)]
 
         slot_word = held.tile([P, PASSES * SLOTS], U32, name="slot_word", tag="tokens", align_bytes=64)
         for c0 in range(0, SLOTS, GATHER):
@@ -199,7 +201,7 @@ def tile_moe_ecr_glu_gelu_kernel(tc, x_words, x_scales, w1_words, w1_scales, w3_
                 h_word, h_plane = quantised[e]
                 nc.tensor.matmul_mx(
                     out=bank[:, m * C : (m + 1) * C],
-                    lhsT=w2[:, e, :].bitcast(FP4X4),
+                    lhsT=w2[e // HALF][:, e % HALF, :].bitcast(FP4X4),
                     lhsT_scale=w2_plane[:, e, :],
                     rhs=h_word.bitcast(FP8X4),
                     rhs_scale=h_plane,
@@ -220,6 +222,9 @@ def tile_moe_ecr_glu_gelu_kernel(tc, x_words, x_scales, w1_words, w1_scales, w3_
         turn((5,), banks[1], nc.vector.tensor_copy)
         turn((6,), banks[5])
         turn((7,), banks[4])
+        gate_column = held.tile([P, BLOCKS], F32, name="gate_column")
+        nc.tensor.transpose(banks[3][:, :P], gate_rows[:], identity[:])
+        nc.scalar.copy(out=gate_column[:], in_=banks[3][:, :BLOCKS])
         second((0, 1, 2, 3), banks[2], nc.scalar.copy)
         second((4, 5, 6), banks[0], nc.vector.tensor_copy)
         second((7,), banks[7], nc.scalar.copy)
@@ -229,44 +234,39 @@ def tile_moe_ecr_glu_gelu_kernel(tc, x_words, x_scales, w1_words, w1_scales, w3_
 
         def gated(r, t0, t1):
             term = held.tile([P, t1 - t0], F32, name=f"term{r}_{t0}")
-            nc.vector.tensor_tensor(term[:], picked(r, t0, t1), gates[r][:, t0:t1], MULT)
+            nc.vector.tensor_tensor(term[:], picked(r, t0, t1), gates[r, t0][:], MULT)
             return term
 
-        def fetch(c):
-            t0 = c * CHUNK
-            plain = held.tile([P, CHUNK], F32, name=f"plain{c}")
-            nc.scalar.activation(out=plain[:], in_=picked(2, t0, t0 + CHUNK), func=COPY)
-            for b0 in range(0, CHUNK, P):
-                nc.tensor.transpose(banks[1 + c][:, b0 : b0 + P], plain[:, b0 : b0 + P], identity[:])
+        def by_token(term, bank):
+            for b0 in range(0, term.shape[1], P):
+                nc.tensor.transpose(bank[:, b0 : b0 + P], term[:, b0 : b0 + P], identity[:])
+            return bank[:, : term.shape[1]]
 
-        def weigh(c, extra=None):
-            t0 = c * CHUNK
-            parts = [held.tile([P, CHUNK], F32, name=f"by_token{c}")]
-            for b0 in range(0, CHUNK, P):
-                b = GATE_ROW[2 * BLOCKS + (t0 + b0) // P]
-                nc.scalar.activation(out=parts[0][:, b0 : b0 + P], in_=banks[1 + c][:, b0 : b0 + P], func=COPY, scale=gate_column[:, b : b + 1])
-            if extra is not None:
-                parts.append(held.tile([P, CHUNK], F32, name="extra_by_token"))
-                nc.scalar.copy(out=parts[1][:], in_=extra)
-            for b0 in range(0, CHUNK, P):
+        third, second_turned = [], []
+        for c, (t0, t1) in enumerate(CHUNKS):
+            plain = held.tile([P, t1 - t0], F32, name=f"plain{c}")
+            nc.scalar.activation(out=plain[:], in_=picked(2, t0, t1), func=COPY)
+            third.append(by_token(plain, banks[1 + c]))
+            if c < TURNED:
+                second_turned.append(by_token(gated(1, t0, t1), banks[7 * c]))
+        for c, (t0, t1) in enumerate(CHUNKS):
+            parts = [held.tile([P, t1 - t0], F32, name=f"third{c}")]
+            for b0 in range(0, t1 - t0, P):
+                k = (t0 + b0) // P
+                nc.scalar.activation(out=parts[0][:, b0 : b0 + P], in_=third[c][:, b0 : b0 + P], func=COPY, scale=gate_column[:, k : k + 1])
+            if c < TURNED:
+                parts.append(held.tile([P, t1 - t0], F32, name=f"second{c}"))
+                nc.scalar.copy(out=parts[1][:], in_=second_turned[c])
+            for b0 in range(0, t1 - t0, P):
                 for n, part in enumerate(parts):
                     nc.tensor.matmul(banks[4 + c][:, b0 : b0 + P], lhsT=part[:, b0 : b0 + P], rhs=identity[:], is_transpose=True, start=(n == 0), stop=(n == len(parts) - 1))
-
-        fetch(0)
-        first2 = gated(1, 0, CHUNK)
-        for b0 in range(0, CHUNK, P):
-            nc.tensor.transpose(banks[0][:, b0 : b0 + P], first2[:, b0 : b0 + P], identity[:])
-        fetch(1)
-        fetch(2)
-        weigh(0, banks[0][:, :CHUNK])
-        weigh(1)
-        weigh(2)
-        rest2 = gated(1, CHUNK, T)
-        rest1 = gated(0, CHUNK, T)
-        first1 = gated(0, 0, CHUNK)
-        rest = held.tile([P, T - CHUNK], F32, name="rest")
-        nc.vector.tensor_tensor(rest[:], rest2[:], rest1[:], ADD)
-        for c, term in enumerate((first1[:], rest[:, :CHUNK], rest[:, CHUNK:])):
-            result = held.tile([P, CHUNK], F32, name=f"result{c}")
-            nc.vector.tensor_tensor(result[:], banks[4 + c][:, :CHUNK], term, ADD)
-            nc.sync.dma_start(out=out[:, c * CHUNK : (c + 1) * CHUNK], in_=result[:])
+        late2 = gated(1, split, T)
+        late1 = gated(0, split, T)
+        early1 = gated(0, 0, split)
+        late = held.tile([P, T - split], F32, name="late")
+        nc.vector.tensor_tensor(late[:], late2[:], late1[:], ADD)
+        for c, (t0, t1) in enumerate(CHUNKS):
+            term = early1[:, t0:t1] if c < TURNED else late[:, t0 - split : t1 - split]
+            result = held.tile([P, t1 - t0], F32, name=f"result{c}")
+            nc.vector.tensor_tensor(result[:], banks[4 + c][:, : t1 - t0], term, ADD)
+            nc.sync.dma_start(out=out[:, t0:t1], in_=result[:])

@@ -42,6 +42,7 @@ def tile_moe_ecr_glu_gelu_kernel(tc, x_words, x_scales, w1_words, w1_scales, w3_
     nc = tc.nc
     with ExitStack() as ctx:
         held = ctx.enter_context(tc.tile_pool(name="held", bufs=1))
+        late_pool = ctx.enter_context(tc.tile_pool(name="late_pool", bufs=1))
         ring = ctx.enter_context(tc.tile_pool(name="ring", bufs=2))
         psum = ctx.enter_context(tc.psum_pool(name="psum", bufs=1))
 
@@ -55,11 +56,16 @@ def tile_moe_ecr_glu_gelu_kernel(tc, x_words, x_scales, w1_words, w1_scales, w3_
         w1_plane = [held.tile([P, HALF * PASSES, H], U8, name=f"w1_plane{g}", align_bytes=64) for g in range(2)]
         w3_plane = [held.tile([P, HALF * PASSES, H], U8, name=f"w3_plane{g}", align_bytes=64) for g in range(2)]
         w2_plane = held.tile([P, E, N], U8, name="w2_plane", align_bytes=64)
-        for plane in (w1_plane[1], w1_plane[0], w3_plane[0], w3_plane[1]):
-            nc.vector.memset(plane[:].bitcast(I32), 0)
         nc.gpsimd.memset(w2_plane[:].bitcast(I32), 0)
         zeros = held.tile([P, PAD], F32, name="zeros")
         nc.vector.memset(zeros[:], 0.0)
+        for plane in (w1_plane[1], w1_plane[0]):
+            nc.vector.memset(plane[:].bitcast(I32), 0)
+        y = late_pool.tile([P, SLOTS + PAD], F32, name="y")
+        nc.scalar.activation(out=y[:, SLOTS:], in_=zeros[:], func=GELU)
+        for plane in w3_plane:
+            words = plane[:].rearrange("p g w -> p (g w)").bitcast(U32).rearrange("p (a b) -> p a b", b=PAD)
+            nc.scalar.copy(out=words, in_=zeros[:].bitcast(U32).unsqueeze(1).to_broadcast(list(words.shape)))
 
         slot_list = held.tile([P, SLOTS // 16], U16, name="slot_list")
         nc.sync.dma_start(slot_list[:], offs)
@@ -124,8 +130,6 @@ def tile_moe_ecr_glu_gelu_kernel(tc, x_words, x_scales, w1_words, w1_scales, w3_
         make_identity(nc, identity[:])
         load_half(nc.gpsimd, w1_plane, w1_scales, 1)
         load_half(nc.gpsimd, w3_plane, w3_scales, 1)
-        y = held.tile([P, SLOTS + PAD], F32, name="y")
-        nc.scalar.activation(out=y[:, SLOTS:], in_=zeros[:], func=GELU)
 
         banks = [psum.tile([P, H], F32, name=f"bank{b}") for b in range(8)]
 

@@ -59,13 +59,12 @@ def tile_moe_ecr_glu_gelu_kernel(tc, x_words, x_scales, w1_words, w1_scales, w3_
         nc.gpsimd.memset(w2_plane[:].bitcast(I32), 0)
         zeros = held.tile([P, PAD], F32, name="zeros")
         nc.vector.memset(zeros[:], 0.0)
-        for plane in (w1_plane[1], w1_plane[0]):
+        for plane in (w1_plane[1], w1_plane[0], w3_plane[0]):
             nc.vector.memset(plane[:].bitcast(I32), 0)
         y = late_pool.tile([P, SLOTS + PAD], F32, name="y")
         nc.scalar.activation(out=y[:, SLOTS:], in_=zeros[:], func=GELU)
-        for plane in w3_plane:
-            words = plane[:].rearrange("p g w -> p (g w)").bitcast(U32).rearrange("p (a b) -> p a b", b=PAD)
-            nc.scalar.copy(out=words, in_=zeros[:].bitcast(U32).unsqueeze(1).to_broadcast(list(words.shape)))
+        words = w3_plane[1][:].rearrange("p g w -> p (g w)").bitcast(U32).rearrange("p (a b) -> p a b", b=PAD)
+        nc.scalar.copy(out=words, in_=zeros[:].bitcast(U32).unsqueeze(1).to_broadcast(list(words.shape)))
 
         slot_list = held.tile([P, SLOTS // 16], U16, name="slot_list")
         nc.sync.dma_start(slot_list[:], offs)

@@ -25,7 +25,10 @@ GELU = mybir.ActivationFunctionType.Gelu_apprx_tanh
 
 GATHER = 256
 HALF = E // 2
-STEPS = ((0,), (1,), (2,), (3,), (4, 5, 6), (7,))
+STEPS = ((0,), (1,), (2,), (3,), (4,), (5, 6, 7))
+W1_PARTS = ((0, HALF), (HALF, E))
+W3_EARLY = 5
+W3_PARTS = ((0, W3_EARLY), (W3_EARLY, E))
 CHUNKS = ((0, 256), (256, 512), (512, 768))
 TURNED = 1
 BLOCKS = T // P
@@ -54,7 +57,7 @@ def tile_moe_ecr_glu_gelu_kernel(tc, x_words, x_scales, w1_words, w1_scales, w3_
         slot_plane = [held.tile([P, SLOTS], U8, name=f"slot_plane{s}", align_bytes=64) for s in range(PASSES)]
         nc.gpsimd.memset(slot_plane[1][:].bitcast(I32), 0)
         w1_plane = [held.tile([P, HALF * PASSES, H], U8, name=f"w1_plane{g}", align_bytes=64) for g in range(2)]
-        w3_plane = [held.tile([P, HALF * PASSES, H], U8, name=f"w3_plane{g}", align_bytes=64) for g in range(2)]
+        w3_plane = [held.tile([P, (e1 - e0) * PASSES, H], U8, name=f"w3_plane{e0}", align_bytes=64) for e0, e1 in W3_PARTS]
         w2_plane = held.tile([P, E, N], U8, name="w2_plane", align_bytes=64)
         nc.gpsimd.memset(w2_plane[:].bitcast(I32), 0)
         zeros = held.tile([P, PAD], F32, name="zeros")
@@ -84,8 +87,12 @@ def tile_moe_ecr_glu_gelu_kernel(tc, x_words, x_scales, w1_words, w1_scales, w3_
             nc.sync.dma_start(out=tile[:].bitcast(I32), in_=words[e].rearrange("s p b -> p s b").bitcast(I32))
             return [tile[:, s, :] for s in range(PASSES)]
 
-        def load_half(queue, planes, scales, g):
-            load_scale_rows(queue, planes[g], scales[g * HALF : (g + 1) * HALF].rearrange("e s q i -> (e s) q i"))
+        def load_part(queue, planes, scales, parts, g):
+            load_scale_rows(queue, planes[g], scales[parts[g][0] : parts[g][1]].rearrange("e s q i -> (e s) q i"))
+
+        def rows_of(planes, parts, e, s):
+            g = int(e >= parts[1][0])
+            return planes[g][:, (e - parts[g][0]) * PASSES + s, :]
 
         def gather_scales():
             nc.vector.tensor_copy(slot_plane[0][:], x_plane[:].indirect(slot_list[:]))
@@ -93,8 +100,8 @@ def tile_moe_ecr_glu_gelu_kernel(tc, x_words, x_scales, w1_words, w1_scales, w3_
                 nc.sync.dma_start(out=slot_plane[1][j:P:32, :].bitcast(I32), in_=slot_plane[0][16 + j : P : 32, :].bitcast(I32))
 
         w1[0] = load_words(w1_words, 0, "w1")
-        load_half(nc.sync, w1_plane, w1_scales, 0)
-        load_half(nc.sync, w3_plane, w3_scales, 0)
+        load_part(nc.sync, w1_plane, w1_scales, W1_PARTS, 0)
+        load_part(nc.sync, w3_plane, w3_scales, W3_PARTS, 0)
         w3[0] = load_words(w3_words, 0, "w3")
         for step in STEPS[1:]:
             for e in step:
@@ -127,8 +134,8 @@ def tile_moe_ecr_glu_gelu_kernel(tc, x_words, x_scales, w1_words, w1_scales, w3_
 
         identity = held.tile([P, P], F32, name="identity")
         make_identity(nc, identity[:])
-        load_half(nc.gpsimd, w1_plane, w1_scales, 1)
-        load_half(nc.gpsimd, w3_plane, w3_scales, 1)
+        load_part(nc.gpsimd, w1_plane, w1_scales, W1_PARTS, 1)
+        load_part(nc.gpsimd, w3_plane, w3_scales, W3_PARTS, 1)
 
         banks = [psum.tile([P, H], F32, name=f"bank{b}") for b in range(8)]
 
@@ -137,7 +144,7 @@ def tile_moe_ecr_glu_gelu_kernel(tc, x_words, x_scales, w1_words, w1_scales, w3_
             for s in range(PASSES):
                 nc.vector.tensor_copy(slot_word[:, s * SLOTS + c0 : s * SLOTS + c0 + GATHER], x_word[:, s, :].indirect(slot_list[:, c0 // 16 : (c0 + GATHER) // 16]))
 
-        def first_product(e, words, plane, acc):
+        def first_product(e, words, planes, parts, acc):
             slots = slice(e * C, (e + 1) * C)
             for s in range(PASSES):
                 nc.tensor.matmul_mx(
@@ -145,14 +152,14 @@ def tile_moe_ecr_glu_gelu_kernel(tc, x_words, x_scales, w1_words, w1_scales, w3_
                     lhsT=slot_word[:, s * SLOTS + e * C : s * SLOTS + (e + 1) * C].bitcast(FP8X4),
                     lhsT_scale=slot_plane[s][:, slots],
                     rhs=words[s].bitcast(FP4X4),
-                    rhs_scale=plane[e // HALF][:, e % HALF * PASSES + s, :],
+                    rhs_scale=rows_of(planes, parts, e, s),
                     start=(s == 0),
                     stop=(s == PASSES - 1),
                 )
             return acc[:].rearrange("c (p u v) -> c u p v", u=2, v=2)
 
         def activate(e):
-            a = first_product(e, w1[e], w1_plane, banks[e % 2])
+            a = first_product(e, w1[e], w1_plane, W1_PARTS, banks[e % 2])
             act = ring.tile([P, 2, P, 2], F32, name="act", bufs=5)
             nc.scalar.activation(out=act[:], in_=a, func=GELU)
             return act
@@ -167,7 +174,7 @@ def tile_moe_ecr_glu_gelu_kernel(tc, x_words, x_scales, w1_words, w1_scales, w3_
                             lhsT=slot_word[:, s * SLOTS + e * C : s * SLOTS + (e + 1) * C].bitcast(FP8X4),
                             lhsT_scale=slot_plane[s][:, e * C : (e + 1) * C],
                             rhs=w3[e][m][:, s, 2 * c0 : 2 * (c0 + P)].bitcast(FP4X4),
-                            rhs_scale=w3_plane[1][:, e % HALF * PASSES + s, m * H // 2 + c0 : m * H // 2 + c0 + P],
+                            rhs_scale=rows_of(w3_plane, W3_PARTS, e, s)[:, m * H // 2 + c0 : m * H // 2 + c0 + P],
                             start=(s == 0),
                             stop=(s == PASSES - 1),
                         )
@@ -177,19 +184,19 @@ def tile_moe_ecr_glu_gelu_kernel(tc, x_words, x_scales, w1_words, w1_scales, w3_
             hs[e] = [h[:, u] for u in range(2)]
 
         def multiply(e, act):
-            b = first_product(e, w3[e], w3_plane, banks[2 + e % 5])
+            b = first_product(e, w3[e], w3_plane, W3_PARTS, banks[2 + e % 5])
             h = ring.tile([P, 2, P, 2], BF16, name="h", bufs=8)
             nc.vector.tensor_tensor(out=h[:], in0=b, in1=act[:], op=MULT)
             hs[e] = [h[:, u] for u in range(2)]
 
-        def turn(group, bank, copy=nc.scalar.copy):
+        def turn(group, bank):
             width = len(group) * C
             turned = bank[:, : 2 * width].rearrange("p (m u c) -> p m u c", u=2, c=C)
             for m, e in enumerate(group):
                 for u in range(2):
                     nc.tensor.transpose(turned[:, m, u, :], hs[e][u].rearrange("c p v -> c (p v)").bitcast(F32), identity[:])
             grouped = ring.tile([P, 4 * width], BF16, name="grouped", bufs=3, align_bytes=64)
-            copy(
+            nc.scalar.copy(
                 out=grouped[:].bitcast(F32).rearrange("p (m c u) -> p m c u", c=C, u=2),
                 in_=turned.rearrange("p m u c -> p m c u"),
             )
@@ -220,9 +227,8 @@ def tile_moe_ecr_glu_gelu_kernel(tc, x_words, x_scales, w1_words, w1_scales, w3_
                 (multiply if e < E - 1 else multiply_last)(e, act)
             if step[0] in (2, 4):
                 turn((step[0] - 2, step[0] - 1), banks[7])
-            if step[0] == 4:
-                turn((4,), banks[7])
-        turn((5,), banks[1], nc.vector.tensor_copy)
+        turn((4,), banks[7])
+        turn((5,), banks[1])
         turn((6,), banks[5])
         turn((7,), banks[4])
         gate_column = held.tile([P, BLOCKS], F32, name="gate_column")

@@ -23,7 +23,7 @@ MULT = mybir.AluOpType.mult
 ADD = mybir.AluOpType.add
 GELU = mybir.ActivationFunctionType.Gelu_apprx_tanh
 
-GATHER = 256
+GATHERS = ((0, 512), (512, 1024))
 HALF = E // 2
 STEPS = ((0,), (1,), (2,), (3,), (4,), (5, 6, 7))
 W1_PARTS = ((0, HALF), (HALF, E))
@@ -47,6 +47,7 @@ def tile_moe_ecr_glu_gelu_kernel(tc, x_words, x_scales, w1_words, w1_scales, w3_
         held = ctx.enter_context(tc.tile_pool(name="held", bufs=1))
         late_pool = ctx.enter_context(tc.tile_pool(name="late_pool", bufs=1))
         ring = ctx.enter_context(tc.tile_pool(name="ring", bufs=2))
+        lists = ctx.enter_context(tc.tile_pool(name="lists", bufs=1))
         psum = ctx.enter_context(tc.psum_pool(name="psum", bufs=1))
 
         x_plane = held.tile([P, 2 * T], U8, name="x_plane", tag="tokens", align_bytes=64)
@@ -102,6 +103,9 @@ def tile_moe_ecr_glu_gelu_kernel(tc, x_words, x_scales, w1_words, w1_scales, w3_
         w1[0] = load_words(w1_words, 0, "w1")
         load_part(nc.sync, w1_plane, w1_scales, W1_PARTS, 0)
         load_part(nc.sync, w3_plane, w3_scales, W3_PARTS, 0)
+        token_lists = [lists.tile([P, T // 16], U16, name=f"token_list{r}") for r in range(TOP)]
+        for token_list, pos in zip(token_lists, (pos1, pos2, pos3)):
+            nc.sync.dma_start(token_list[:], pos)
         w3[0] = load_words(w3_words, 0, "w3")
         for step in STEPS[1:]:
             for e in step:
@@ -116,7 +120,6 @@ def tile_moe_ecr_glu_gelu_kernel(tc, x_words, x_scales, w1_words, w1_scales, w3_
         for g in range(2):
             nc.sync.dma_start(out=w2[g][:].bitcast(I32), in_=w2_words[g * HALF : (g + 1) * HALF].rearrange("e s p b -> p (e s) b").bitcast(I32))
 
-        token_lists = [held.tile([P, T // 16], U16, name=f"token_list{r}") for r in range(TOP)]
         split = CHUNKS[TURNED][0]
         gates = {}
 
@@ -124,11 +127,8 @@ def tile_moe_ecr_glu_gelu_kernel(tc, x_words, x_scales, w1_words, w1_scales, w3_
             gates[r, t0] = held.tile([P, t1 - t0], F32, name=f"gate{r}_{t0}")
             nc.sync.dma_start(out=gates[r, t0][:], in_=gate[r][:, t0:t1])
 
-        nc.sync.dma_start(token_lists[2][:], pos3)
-        nc.sync.dma_start(token_lists[1][:], pos2)
         load_gate(1, 0, split)
         load_gate(1, split, T)
-        nc.sync.dma_start(token_lists[0][:], pos1)
         load_gate(0, split, T)
         load_gate(0, 0, split)
 
@@ -140,9 +140,9 @@ def tile_moe_ecr_glu_gelu_kernel(tc, x_words, x_scales, w1_words, w1_scales, w3_
         banks = [psum.tile([P, H], F32, name=f"bank{b}") for b in range(8)]
 
         slot_word = held.tile([P, PASSES * SLOTS], U32, name="slot_word", tag="tokens", align_bytes=64)
-        for c0 in range(0, SLOTS, GATHER):
+        for c0, c1 in GATHERS:
             for s in range(PASSES):
-                nc.vector.tensor_copy(slot_word[:, s * SLOTS + c0 : s * SLOTS + c0 + GATHER], x_word[:, s, :].indirect(slot_list[:, c0 // 16 : (c0 + GATHER) // 16]))
+                nc.vector.tensor_copy(slot_word[:, s * SLOTS + c0 : s * SLOTS + c1], x_word[:, s, :].indirect(slot_list[:, c0 // 16 : c1 // 16]))
 
         def first_product(e, words, planes, parts, acc):
             slots = slice(e * C, (e + 1) * C)

@@ -25,13 +25,14 @@ GELU = mybir.ActivationFunctionType.Gelu_apprx_tanh
 
 GATHERS = ((0, 512), (512, 1024))
 HALF = E // 2
-STEPS = ((0,), (1,), (2,), (3,), (4,), (5, 6, 7))
-W1_PARTS = ((0, HALF), (HALF, E))
-W3_EARLY = 5
+W1_EARLY = 2
+W1_PARTS = ((0, W1_EARLY), (W1_EARLY, E))
+W3_EARLY = 4
 W3_PARTS = ((0, W3_EARLY), (W3_EARLY, E))
 CHUNKS = ((0, 256), (256, 512), (512, 768))
 TURNED = 1
 BLOCKS = T // P
+A_BANK = (0, 1, 6, 0, 7, 1, 0, 1)
 COPY = mybir.ActivationFunctionType.Copy
 
 
@@ -50,30 +51,28 @@ def tile_moe_ecr_glu_gelu_kernel(tc, x_words, x_scales, w1_words, w1_scales, w3_
         lists = ctx.enter_context(tc.tile_pool(name="lists", bufs=1))
         psum = ctx.enter_context(tc.psum_pool(name="psum", bufs=1))
 
+        w1_plane = [held.tile([P, (e1 - e0) * PASSES, H], U8, name=f"w1_plane{e0}", align_bytes=64) for e0, e1 in W1_PARTS]
+        w3_plane = [held.tile([P, (e1 - e0) * PASSES, H], U8, name=f"w3_plane{e0}", align_bytes=64) for e0, e1 in W3_PARTS]
+        w2_plane = held.tile([P, E, N], U8, name="w2_plane", align_bytes=64)
         x_plane = held.tile([P, 2 * T], U8, name="x_plane", tag="tokens", align_bytes=64)
-        nc.vector.memset(x_plane[:].bitcast(I32), 0)
+        slot_plane = [held.tile([P, SLOTS], U8, name=f"slot_plane{s}", align_bytes=64) for s in range(PASSES)]
+        zeros = held.tile([P, PAD], F32, name="zeros")
+        for plane in (w1_plane[0], x_plane):
+            nc.vector.memset(plane[:].bitcast(I32), 0)
+        nc.vector.memset(zeros[:], 0.0)
+        for plane in (w3_plane[0], slot_plane[1], w1_plane[1]):
+            nc.vector.memset(plane[:].bitcast(I32), 0)
         x_rows = x_scales.rearrange("s (q j) t -> j q s t", j=4)
         for j in range(4):
             nc.scalar.dma_start(out=x_plane[j:P:16, :T].bitcast(I32), in_=x_rows[j].bitcast(I32))
-        slot_plane = [held.tile([P, SLOTS], U8, name=f"slot_plane{s}", align_bytes=64) for s in range(PASSES)]
-        nc.gpsimd.memset(slot_plane[1][:].bitcast(I32), 0)
-        w1_plane = [held.tile([P, HALF * PASSES, H], U8, name=f"w1_plane{g}", align_bytes=64) for g in range(2)]
-        w3_plane = [held.tile([P, (e1 - e0) * PASSES, H], U8, name=f"w3_plane{e0}", align_bytes=64) for e0, e1 in W3_PARTS]
-        w2_plane = held.tile([P, E, N], U8, name="w2_plane", align_bytes=64)
-        nc.gpsimd.memset(w2_plane[:].bitcast(I32), 0)
-        zeros = held.tile([P, PAD], F32, name="zeros")
-        nc.vector.memset(zeros[:], 0.0)
-        for plane in (w1_plane[1], w1_plane[0], w3_plane[0]):
-            nc.vector.memset(plane[:].bitcast(I32), 0)
         y = late_pool.tile([P, SLOTS + PAD], F32, name="y")
         nc.scalar.activation(out=y[:, SLOTS:], in_=zeros[:], func=GELU)
-        words = w3_plane[1][:].rearrange("p g w -> p (g w)").bitcast(U32).rearrange("p (a b) -> p a b", b=PAD)
-        nc.scalar.copy(out=words, in_=zeros[:].bitcast(U32).unsqueeze(1).to_broadcast(list(words.shape)))
+        for plane in (w3_plane[1], w2_plane):
+            words = plane[:].rearrange("p g w -> p (g w)").bitcast(U32).rearrange("p (a b) -> p a b", b=PAD)
+            nc.scalar.copy(out=words, in_=zeros[:].bitcast(U32).unsqueeze(1).to_broadcast(list(words.shape)))
 
         slot_list = held.tile([P, SLOTS // 16], U16, name="slot_list")
         nc.sync.dma_start(slot_list[:], offs)
-        x_word = held.tile([P, PASSES, T], U32, name="x_word", align_bytes=64)
-        nc.sync.dma_start(out=x_word[:].bitcast(I32), in_=x_words.rearrange("s p t r -> p s (t r)").bitcast(I32))
 
         w2 = [held.tile([P, HALF, 2 * N], U8, name=f"w2_{g}", align_bytes=64) for g in range(2)]
         w1, w3 = {}, {}
@@ -88,6 +87,12 @@ def tile_moe_ecr_glu_gelu_kernel(tc, x_words, x_scales, w1_words, w1_scales, w3_
             nc.sync.dma_start(out=tile[:].bitcast(I32), in_=words[e].rearrange("s p b -> p s b").bitcast(I32))
             return [tile[:, s, :] for s in range(PASSES)]
 
+        def load_w1(e):
+            w1[e] = load_words(w1_words, e, "w1")
+
+        def load_w3(e):
+            w3[e] = load_words(w3_words, e, "w3")
+
         def load_part(queue, planes, scales, parts, g):
             load_scale_rows(queue, planes[g], scales[parts[g][0] : parts[g][1]].rearrange("e s q i -> (e s) q i"))
 
@@ -100,20 +105,26 @@ def tile_moe_ecr_glu_gelu_kernel(tc, x_words, x_scales, w1_words, w1_scales, w3_
             for j in range(4):
                 nc.sync.dma_start(out=slot_plane[1][j:P:32, :].bitcast(I32), in_=slot_plane[0][16 + j : P : 32, :].bitcast(I32))
 
-        w1[0] = load_words(w1_words, 0, "w1")
+        load_w1(0)
+        load_w3(0)
         load_part(nc.sync, w1_plane, w1_scales, W1_PARTS, 0)
         load_part(nc.sync, w3_plane, w3_scales, W3_PARTS, 0)
+        x_word = [held.tile([P, T], U32, name=f"x_word{s}", align_bytes=64) for s in range(PASSES)]
+        for s in range(PASSES):
+            nc.sync.dma_start(out=x_word[s][:].bitcast(I32), in_=x_words[s].rearrange("p t r -> p (t r)").bitcast(I32))
+        load_w1(1)
+        gather_scales()
+        load_w3(1)
+        for e in (2, 3):
+            load_w3(e)
+            load_w1(e)
         token_lists = [lists.tile([P, T // 16], U16, name=f"token_list{r}") for r in range(TOP)]
-        for token_list, pos in zip(token_lists, (pos1, pos2, pos3)):
+        load_w1(4)
+        for e, token_list, pos in zip((5, 6, 7), token_lists, (pos1, pos2, pos3)):
             nc.sync.dma_start(token_list[:], pos)
-        w3[0] = load_words(w3_words, 0, "w3")
-        for step in STEPS[1:]:
-            for e in step:
-                w1[e] = load_words(w1_words, e, "w1")
-            if step == STEPS[1]:
-                gather_scales()
-            for e in step:
-                w3[e] = load_words(w3_words, e, "w3")
+            load_w1(e)
+        for e in range(4, E):
+            load_w3(e)
         gate_rows = held.tile([P, P], F32, name="gate_rows")
         nc.sync.dma_start(out=gate_rows[:], in_=gate[2].rearrange("n (b t) -> (n b) t", t=P)[:P])
         load_scale_rows(nc.sync, w2_plane, w2_scales.rearrange("e s q n -> (e s) q n"))
@@ -142,7 +153,7 @@ def tile_moe_ecr_glu_gelu_kernel(tc, x_words, x_scales, w1_words, w1_scales, w3_
         slot_word = held.tile([P, PASSES * SLOTS], U32, name="slot_word", tag="tokens", align_bytes=64)
         for c0, c1 in GATHERS:
             for s in range(PASSES):
-                nc.vector.tensor_copy(slot_word[:, s * SLOTS + c0 : s * SLOTS + c1], x_word[:, s, :].indirect(slot_list[:, c0 // 16 : c1 // 16]))
+                nc.vector.tensor_copy(slot_word[:, s * SLOTS + c0 : s * SLOTS + c1], x_word[s][:].indirect(slot_list[:, c0 // 16 : c1 // 16]))
 
         def first_product(e, words, planes, parts, acc):
             slots = slice(e * C, (e + 1) * C)
@@ -159,14 +170,14 @@ def tile_moe_ecr_glu_gelu_kernel(tc, x_words, x_scales, w1_words, w1_scales, w3_
             return acc[:].rearrange("c (p u v) -> c u p v", u=2, v=2)
 
         def activate(e):
-            a = first_product(e, w1[e], w1_plane, W1_PARTS, banks[e % 2])
-            act = ring.tile([P, 2, P, 2], F32, name="act", bufs=5)
+            a = first_product(e, w1[e], w1_plane, W1_PARTS, banks[A_BANK[e]])
+            act = ring.tile([P, 2, P, 2], F32, name="act", bufs=8)
             nc.scalar.activation(out=act[:], in_=a, func=GELU)
             return act
 
         def multiply_last(e, act):
             h = held.tile([P, 2, P, 2], BF16, name="h_last")
-            for m, bank in enumerate((banks[4], banks[6])):
+            for m, bank in enumerate((banks[5], banks[6])):
                 for c0 in range(0, H // 2, P):
                     for s in range(PASSES):
                         nc.tensor.matmul_mx(
@@ -183,8 +194,10 @@ def tile_moe_ecr_glu_gelu_kernel(tc, x_words, x_scales, w1_words, w1_scales, w3_
                 nc.vector.tensor_tensor(out=h[:, :, words, :], in0=b, in1=act[:, :, words, :], op=MULT)
             hs[e] = [h[:, u] for u in range(2)]
 
-        def multiply(e, act):
-            b = first_product(e, w3[e], w3_plane, W3_PARTS, banks[2 + e % 5])
+        def linear(e):
+            return first_product(e, w3[e], w3_plane, W3_PARTS, banks[2 + e % 4])
+
+        def multiply(e, act, b):
             h = ring.tile([P, 2, P, 2], BF16, name="h", bufs=8)
             nc.vector.tensor_tensor(out=h[:], in0=b, in1=act[:], op=MULT)
             hs[e] = [h[:, u] for u in range(2)]
@@ -221,21 +234,29 @@ def tile_moe_ecr_glu_gelu_kernel(tc, x_words, x_scales, w1_words, w1_scales, w3_
             copy(out=y[:, experts[0] * C : (experts[-1] + 1) * C], in_=bank[:, : len(experts) * C])
 
         hs, quantised = {}, {}
-        for step in STEPS:
-            acts = [activate(e) for e in step]
-            for e, act in zip(step, acts):
-                (multiply if e < E - 1 else multiply_last)(e, act)
-            if step[0] in (2, 4):
-                turn((step[0] - 2, step[0] - 1), banks[7])
+        for e in (0, 1):
+            act = activate(e)
+            multiply(e, act, linear(e))
+        for e in (2, 3):
+            b = linear(e)
+            multiply(e, activate(e), b)
+        turn((0, 1), banks[6])
+        acts = {4: activate(4)}
+        turn((2, 3), banks[7])
+        for e in (5, 6, 7):
+            acts[e] = activate(e)
+        for e in (4, 5, 6):
+            multiply(e, acts[e], linear(e))
+        multiply_last(7, acts[7])
         turn((4,), banks[7])
-        turn((5,), banks[1])
-        turn((6,), banks[5])
-        turn((7,), banks[4])
+        turn((5,), banks[0])
+        turn((6,), banks[1])
+        turn((7,), banks[2])
         gate_column = held.tile([P, BLOCKS], F32, name="gate_column")
-        nc.tensor.transpose(banks[3][:, :P], gate_rows[:], identity[:])
-        nc.scalar.copy(out=gate_column[:], in_=banks[3][:, :BLOCKS])
-        second((0, 1, 2, 3), banks[2], nc.scalar.copy)
-        second((4, 5, 6), banks[0], nc.vector.tensor_copy)
+        nc.tensor.transpose(banks[0][:, :P], gate_rows[:], identity[:])
+        nc.scalar.copy(out=gate_column[:], in_=banks[0][:, :BLOCKS])
+        second((0, 1, 2, 3), banks[3], nc.scalar.copy)
+        second((4, 5, 6), banks[4], nc.vector.tensor_copy)
         second((7,), banks[7], nc.scalar.copy)
 
         def picked(r, t0, t1):

@@ -25,9 +25,9 @@ GELU = mybir.ActivationFunctionType.Gelu_apprx_tanh
 
 GATHERS = ((0, 512), (512, 1024))
 HALF = E // 2
-W1_EARLY = 2
+W1_EARLY = 4
 W1_PARTS = ((0, W1_EARLY), (W1_EARLY, E))
-W3_EARLY = 4
+W3_EARLY = 5
 W3_PARTS = ((0, W3_EARLY), (W3_EARLY, E))
 CHUNKS = ((0, 256), (256, 512), (512, 768))
 TURNED = 1
@@ -52,24 +52,25 @@ def tile_moe_ecr_glu_gelu_kernel(tc, x_words, x_scales, w1_words, w1_scales, w3_
         psum = ctx.enter_context(tc.psum_pool(name="psum", bufs=1))
 
         w1_plane = [held.tile([P, (e1 - e0) * PASSES, H], U8, name=f"w1_plane{e0}", align_bytes=64) for e0, e1 in W1_PARTS]
-        w3_plane = [held.tile([P, (e1 - e0) * PASSES, H], U8, name=f"w3_plane{e0}", align_bytes=64) for e0, e1 in W3_PARTS]
+        w3_plane = [held.tile([P, W3_EARLY * PASSES, H], U8, name="w3_early", align_bytes=64)]
         w2_plane = held.tile([P, E, N], U8, name="w2_plane", align_bytes=64)
         x_plane = held.tile([P, 2 * T], U8, name="x_plane", tag="tokens", align_bytes=64)
         slot_plane = [held.tile([P, SLOTS], U8, name=f"slot_plane{s}", align_bytes=64) for s in range(PASSES)]
         zeros = held.tile([P, PAD], F32, name="zeros")
-        for plane in (w1_plane[0], x_plane):
-            nc.vector.memset(plane[:].bitcast(I32), 0)
+        nc.vector.memset(x_plane[:].bitcast(I32), 0)
         nc.vector.memset(zeros[:], 0.0)
-        for plane in (w3_plane[0], slot_plane[1], w1_plane[1]):
-            nc.vector.memset(plane[:].bitcast(I32), 0)
-        x_rows = x_scales.rearrange("s (q j) t -> j q s t", j=4)
-        for j in range(4):
-            nc.scalar.dma_start(out=x_plane[j:P:16, :T].bitcast(I32), in_=x_rows[j].bitcast(I32))
+        nc.vector.memset(slot_plane[1][:].bitcast(I32), 0)
+
+        def clear(copy, plane, dtype):
+            words = plane[:].rearrange("p g w -> p (g w)").bitcast(dtype).rearrange("p (a b) -> p a b", b=PAD)
+            copy(out=words, in_=zeros[:].bitcast(dtype).unsqueeze(1).to_broadcast(list(words.shape)))
+
+        for plane in (w1_plane[0], w3_plane[0]):
+            clear(nc.vector.tensor_copy, plane, I32)
         y = late_pool.tile([P, SLOTS + PAD], F32, name="y")
         nc.scalar.activation(out=y[:, SLOTS:], in_=zeros[:], func=GELU)
-        for plane in (w3_plane[1], w2_plane):
-            words = plane[:].rearrange("p g w -> p (g w)").bitcast(U32).rearrange("p (a b) -> p a b", b=PAD)
-            nc.scalar.copy(out=words, in_=zeros[:].bitcast(U32).unsqueeze(1).to_broadcast(list(words.shape)))
+        for plane in (w1_plane[1], w2_plane):
+            clear(nc.scalar.copy, plane, U32)
 
         slot_list = held.tile([P, SLOTS // 16], U16, name="slot_list")
         nc.sync.dma_start(slot_list[:], offs)
@@ -106,24 +107,24 @@ def tile_moe_ecr_glu_gelu_kernel(tc, x_words, x_scales, w1_words, w1_scales, w3_
                 nc.sync.dma_start(out=slot_plane[1][j:P:32, :].bitcast(I32), in_=slot_plane[0][16 + j : P : 32, :].bitcast(I32))
 
         load_w1(0)
-        load_w3(0)
+        x_rows = x_scales.rearrange("s (q j) t -> j q s t", j=4)
+        for j in range(4):
+            nc.sync.dma_start(out=x_plane[j:P:16, :T].bitcast(I32), in_=x_rows[j].bitcast(I32))
+        x_word = held.tile([P, PASSES, T], U32, name="x_word", tag="token_words", align_bytes=64)
+        nc.sync.dma_start(out=x_word[:].bitcast(I32), in_=x_words.rearrange("s p t r -> p s (t r)").bitcast(I32))
         load_part(nc.sync, w1_plane, w1_scales, W1_PARTS, 0)
         load_part(nc.sync, w3_plane, w3_scales, W3_PARTS, 0)
-        x_word = [held.tile([P, T], U32, name=f"x_word{s}", align_bytes=64) for s in range(PASSES)]
-        for s in range(PASSES):
-            nc.sync.dma_start(out=x_word[s][:].bitcast(I32), in_=x_words[s].rearrange("p t r -> p (t r)").bitcast(I32))
-        load_w1(1)
         gather_scales()
-        load_w3(1)
-        for e in (2, 3):
+        load_part(nc.sync, w1_plane, w1_scales, W1_PARTS, 1)
+        load_w3(0)
+        for e in range(1, W3_EARLY):
+            load_w1(e)
             load_w3(e)
-            load_w1(e)
         token_lists = [lists.tile([P, T // 16], U16, name=f"token_list{r}") for r in range(TOP)]
-        load_w1(4)
-        for e, token_list, pos in zip((5, 6, 7), token_lists, (pos1, pos2, pos3)):
-            nc.sync.dma_start(token_list[:], pos)
+        for e, token_list, pos in zip(range(W3_EARLY, E), token_lists, (pos1, pos2, pos3)):
             load_w1(e)
-        for e in range(4, E):
+            nc.sync.dma_start(token_list[:], pos)
+        for e in range(W3_EARLY, E):
             load_w3(e)
         gate_rows = held.tile([P, P], F32, name="gate_rows")
         nc.sync.dma_start(out=gate_rows[:], in_=gate[2].rearrange("n (b t) -> (n b) t", t=P)[:P])
@@ -145,15 +146,16 @@ def tile_moe_ecr_glu_gelu_kernel(tc, x_words, x_scales, w1_words, w1_scales, w3_
 
         identity = held.tile([P, P], F32, name="identity")
         make_identity(nc, identity[:])
-        load_part(nc.gpsimd, w1_plane, w1_scales, W1_PARTS, 1)
-        load_part(nc.gpsimd, w3_plane, w3_scales, W3_PARTS, 1)
 
         banks = [psum.tile([P, H], F32, name=f"bank{b}") for b in range(8)]
 
         slot_word = held.tile([P, PASSES * SLOTS], U32, name="slot_word", tag="tokens", align_bytes=64)
         for c0, c1 in GATHERS:
             for s in range(PASSES):
-                nc.vector.tensor_copy(slot_word[:, s * SLOTS + c0 : s * SLOTS + c1], x_word[s][:].indirect(slot_list[:, c0 // 16 : c1 // 16]))
+                nc.vector.tensor_copy(slot_word[:, s * SLOTS + c0 : s * SLOTS + c1], x_word[:, s, :].indirect(slot_list[:, c0 // 16 : c1 // 16]))
+
+        w3_plane.append(held.tile([P, (E - W3_EARLY) * PASSES, H], U8, name="w3_late", tag="token_words", align_bytes=64))
+        load_part(nc.gpsimd, w3_plane, w3_scales, W3_PARTS, 1)
 
         def first_product(e, words, planes, parts, acc):
             slots = slice(e * C, (e + 1) * C)
@@ -177,7 +179,7 @@ def tile_moe_ecr_glu_gelu_kernel(tc, x_words, x_scales, w1_words, w1_scales, w3_
 
         def multiply_last(e, act):
             h = held.tile([P, 2, P, 2], BF16, name="h_last")
-            for m, bank in enumerate((banks[5], banks[6])):
+            for m, bank in enumerate((banks[5], banks[2])):
                 for c0 in range(0, H // 2, P):
                     for s in range(PASSES):
                         nc.tensor.matmul_mx(
@@ -234,27 +236,26 @@ def tile_moe_ecr_glu_gelu_kernel(tc, x_words, x_scales, w1_words, w1_scales, w3_
             copy(out=y[:, experts[0] * C : (experts[-1] + 1) * C], in_=bank[:, : len(experts) * C])
 
         hs, quantised = {}, {}
-        for e in (0, 1):
+        for e in (0, 1, 2):
             act = activate(e)
             multiply(e, act, linear(e))
-        for e in (2, 3):
-            b = linear(e)
-            multiply(e, activate(e), b)
         turn((0, 1), banks[6])
-        acts = {4: activate(4)}
+        act = activate(3)
+        multiply(3, act, linear(3))
+        act = activate(4)
+        multiply(4, act, linear(4))
         turn((2, 3), banks[7])
-        for e in (5, 6, 7):
-            acts[e] = activate(e)
-        for e in (4, 5, 6):
+        acts = {e: activate(e) for e in (5, 6, 7)}
+        turn((4,), banks[6])
+        for e in (5, 6):
             multiply(e, acts[e], linear(e))
         multiply_last(7, acts[7])
-        turn((4,), banks[7])
-        turn((5,), banks[0])
-        turn((6,), banks[1])
-        turn((7,), banks[2])
+        turn((5,), banks[7])
+        turn((6,), banks[0])
+        turn((7,), banks[1])
         gate_column = held.tile([P, BLOCKS], F32, name="gate_column")
-        nc.tensor.transpose(banks[0][:, :P], gate_rows[:], identity[:])
-        nc.scalar.copy(out=gate_column[:], in_=banks[0][:, :BLOCKS])
+        nc.tensor.transpose(banks[6][:, :P], gate_rows[:], identity[:])
+        nc.scalar.copy(out=gate_column[:], in_=banks[6][:, :BLOCKS])
         second((0, 1, 2, 3), banks[3], nc.scalar.copy)
         second((4, 5, 6), banks[4], nc.vector.tensor_copy)
         second((7,), banks[7], nc.scalar.copy)

@@ -51,11 +51,11 @@ def tile_moe_ecr_glu_gelu_kernel(tc, x_words, x_scales, w1_words, w1_scales, w3_
         lists = ctx.enter_context(tc.tile_pool(name="lists", bufs=1))
         psum = ctx.enter_context(tc.psum_pool(name="psum", bufs=1))
 
-        w1_plane = [held.tile([P, (e1 - e0) * PASSES, H], U8, name=f"w1_plane{e0}", align_bytes=64) for e0, e1 in W1_PARTS]
-        w3_plane = [held.tile([P, W3_EARLY * PASSES, H], U8, name="w3_early", align_bytes=64)]
-        w2_plane = held.tile([P, E, N], U8, name="w2_plane", align_bytes=64)
-        x_plane = held.tile([P, 2 * T], U8, name="x_plane", tag="tokens", align_bytes=64)
-        slot_plane = [held.tile([P, SLOTS], U8, name=f"slot_plane{s}", align_bytes=64) for s in range(PASSES)]
+        w1_plane = [held.tile([P, (e1 - e0) * PASSES, H], U8, name=f"w1_plane{e0}", align_bytes=256) for e0, e1 in W1_PARTS]
+        w3_plane = [held.tile([P, W3_EARLY * PASSES, H], U8, name="w3_early", align_bytes=256)]
+        w2_plane = held.tile([P, E, N], U8, name="w2_plane", align_bytes=256)
+        x_plane = held.tile([P, 2 * T], U8, name="x_plane", tag="tokens", align_bytes=256)
+        slot_plane = [held.tile([P, SLOTS], U8, name=f"slot_plane{s}", align_bytes=256) for s in range(PASSES)]
         zeros = held.tile([P, PAD], F32, name="zeros")
         nc.vector.memset(x_plane[:].bitcast(I32), 0)
         nc.vector.memset(zeros[:], 0.0)
@@ -75,16 +75,16 @@ def tile_moe_ecr_glu_gelu_kernel(tc, x_words, x_scales, w1_words, w1_scales, w3_
         slot_list = held.tile([P, SLOTS // 16], U16, name="slot_list")
         nc.sync.dma_start(slot_list[:], offs)
 
-        w2 = [held.tile([P, HALF, 2 * N], U8, name=f"w2_{g}", align_bytes=64) for g in range(2)]
+        w2 = [held.tile([P, HALF, 2 * N], U8, name=f"w2_{g}", align_bytes=256) for g in range(2)]
         w1, w3 = {}, {}
 
         def load_words(words, e, name):
             if (name, e) == ("w3", E - 1):
-                halves = [held.tile([P, PASSES, H], U8, name=f"{name}_{e}_{m}", align_bytes=64) for m in range(2)]
+                halves = [held.tile([P, PASSES, H], U8, name=f"{name}_{e}_{m}", align_bytes=256) for m in range(2)]
                 for m in range(2):
                     nc.sync.dma_start(out=halves[m][:].bitcast(I32), in_=words[e].rearrange("s p b -> p s b")[:, :, m * H : (m + 1) * H].bitcast(I32))
                 return halves
-            tile = held.tile([P, PASSES, 2 * H], U8, name=f"{name}_{e}", align_bytes=64)
+            tile = held.tile([P, PASSES, 2 * H], U8, name=f"{name}_{e}", align_bytes=256)
             nc.sync.dma_start(out=tile[:].bitcast(I32), in_=words[e].rearrange("s p b -> p s b").bitcast(I32))
             return [tile[:, s, :] for s in range(PASSES)]
 
@@ -110,7 +110,7 @@ def tile_moe_ecr_glu_gelu_kernel(tc, x_words, x_scales, w1_words, w1_scales, w3_
         x_rows = x_scales.rearrange("s (q j) t -> j q s t", j=4)
         for j in range(4):
             nc.sync.dma_start(out=x_plane[j:P:16, :T].bitcast(I32), in_=x_rows[j].bitcast(I32))
-        x_word = held.tile([P, PASSES, T], U32, name="x_word", tag="token_words", align_bytes=64)
+        x_word = held.tile([P, PASSES, T], U32, name="x_word", tag="token_words", align_bytes=256)
         nc.sync.dma_start(out=x_word[:].bitcast(I32), in_=x_words.rearrange("s p t r -> p s (t r)").bitcast(I32))
         load_part(nc.sync, w1_plane, w1_scales, W1_PARTS, 0)
         load_part(nc.sync, w3_plane, w3_scales, W3_PARTS, 0)
@@ -126,7 +126,7 @@ def tile_moe_ecr_glu_gelu_kernel(tc, x_words, x_scales, w1_words, w1_scales, w3_
             nc.sync.dma_start(token_list[:], pos)
         for e in range(W3_EARLY, E):
             load_w3(e)
-        gate_rows = held.tile([P, P], F32, name="gate_rows")
+        gate_rows = held.tile([P, P], F32, name="gate_rows", align_bytes=256)
         nc.sync.dma_start(out=gate_rows[:], in_=gate[2].rearrange("n (b t) -> (n b) t", t=P)[:P])
         load_scale_rows(nc.sync, w2_plane, w2_scales.rearrange("e s q n -> (e s) q n"))
         for g in range(2):
@@ -136,7 +136,7 @@ def tile_moe_ecr_glu_gelu_kernel(tc, x_words, x_scales, w1_words, w1_scales, w3_
         gates = {}
 
         def load_gate(r, t0, t1):
-            gates[r, t0] = held.tile([P, t1 - t0], F32, name=f"gate{r}_{t0}")
+            gates[r, t0] = held.tile([P, t1 - t0], F32, name=f"gate{r}_{t0}", align_bytes=256)
             nc.sync.dma_start(out=gates[r, t0][:], in_=gate[r][:, t0:t1])
 
         load_gate(1, 0, split)
@@ -149,12 +149,12 @@ def tile_moe_ecr_glu_gelu_kernel(tc, x_words, x_scales, w1_words, w1_scales, w3_
 
         banks = [psum.tile([P, H], F32, name=f"bank{b}") for b in range(8)]
 
-        slot_word = held.tile([P, PASSES * SLOTS], U32, name="slot_word", tag="tokens", align_bytes=64)
+        slot_word = held.tile([P, PASSES * SLOTS], U32, name="slot_word", tag="tokens", align_bytes=256)
         for c0, c1 in GATHERS:
             for s in range(PASSES):
                 nc.vector.tensor_copy(slot_word[:, s * SLOTS + c0 : s * SLOTS + c1], x_word[:, s, :].indirect(slot_list[:, c0 // 16 : c1 // 16]))
 
-        w3_plane.append(held.tile([P, (E - W3_EARLY) * PASSES, H], U8, name="w3_late", tag="token_words", align_bytes=64))
+        w3_plane.append(held.tile([P, (E - W3_EARLY) * PASSES, H], U8, name="w3_late", tag="token_words", align_bytes=256))
         load_part(nc.gpsimd, w3_plane, w3_scales, W3_PARTS, 1)
 
         def first_product(e, words, planes, parts, acc):
@@ -210,13 +210,13 @@ def tile_moe_ecr_glu_gelu_kernel(tc, x_words, x_scales, w1_words, w1_scales, w3_
             for m, e in enumerate(group):
                 for u in range(2):
                     nc.tensor.transpose(turned[:, m, u, :], hs[e][u].rearrange("c p v -> c (p v)").bitcast(F32), identity[:])
-            grouped = ring.tile([P, 4 * width], BF16, name="grouped", bufs=3, align_bytes=64)
+            grouped = ring.tile([P, 4 * width], BF16, name="grouped", bufs=3, align_bytes=256)
             nc.scalar.copy(
                 out=grouped[:].bitcast(F32).rearrange("p (m c u) -> p m c u", c=C, u=2),
                 in_=turned.rearrange("p m u c -> p m c u"),
             )
-            h_word = held.tile([P, width], U32, name=f"h_word{group[0]}", align_bytes=64)
-            h_plane = held.tile([P, width], U8, name=f"h_plane{group[0]}", align_bytes=64)
+            h_word = held.tile([P, width], U32, name=f"h_word{group[0]}", align_bytes=256)
+            h_plane = held.tile([P, width], U8, name=f"h_plane{group[0]}", align_bytes=256)
             nc.vector.quantize_mx(out=h_word[:].bitcast(FP8X4), scales=h_plane[:], in_=grouped[:])
             for m, e in enumerate(group):
                 quantised[e] = (h_word[:, m * C : (m + 1) * C], h_plane[:, m * C : (m + 1) * C])
@@ -298,6 +298,6 @@ def tile_moe_ecr_glu_gelu_kernel(tc, x_words, x_scales, w1_words, w1_scales, w3_
         nc.vector.tensor_tensor(late[:], late2[:], late1[:], ADD)
         for c, (t0, t1) in enumerate(CHUNKS):
             term = early1[:, t0:t1] if c < TURNED else late[:, t0 - split : t1 - split]
-            result = held.tile([P, t1 - t0], F32, name=f"result{c}")
+            result = held.tile([P, t1 - t0], F32, name=f"result{c}", align_bytes=256)
             nc.vector.tensor_tensor(result[:], banks[4 + c][:, : t1 - t0], term, ADD)
             nc.sync.dma_start(out=out[:, t0:t1], in_=result[:])

@@ -73,7 +73,6 @@ def tile_moe_ecr_glu_gelu_kernel(tc, x_words, x_scales, w1_words, w1_scales, w3_
             clear(nc.scalar.copy, plane, U32)
 
         slot_list = held.tile([P, SLOTS // 16], U16, name="slot_list")
-        nc.sync.dma_start(slot_list[:], offs)
 
         w2 = [held.tile([P, HALF, 2 * N], U8, name=f"w2_{g}", align_bytes=256) for g in range(2)]
         w1, w3 = {}, {}
@@ -107,17 +106,20 @@ def tile_moe_ecr_glu_gelu_kernel(tc, x_words, x_scales, w1_words, w1_scales, w3_
                 nc.sync.dma_start(out=slot_plane[1][j:P:32, :].bitcast(I32), in_=slot_plane[0][16 + j : P : 32, :].bitcast(I32))
 
         load_w1(0)
+        nc.sync.dma_start(slot_list[:], offs)
         x_rows = x_scales.rearrange("s (q j) t -> j q s t", j=4)
         for j in range(4):
             nc.sync.dma_start(out=x_plane[j:P:16, :T].bitcast(I32), in_=x_rows[j].bitcast(I32))
         x_word = held.tile([P, PASSES, T], U32, name="x_word", tag="token_words", align_bytes=256)
         nc.sync.dma_start(out=x_word[:].bitcast(I32), in_=x_words.rearrange("s p t r -> p s (t r)").bitcast(I32))
-        load_part(nc.sync, w1_plane, w1_scales, W1_PARTS, 0)
-        load_part(nc.sync, w3_plane, w3_scales, W3_PARTS, 0)
-        gather_scales()
-        load_part(nc.sync, w1_plane, w1_scales, W1_PARTS, 1)
+        load_w1(1)
         load_w3(0)
-        for e in range(1, W3_EARLY):
+        load_part(nc.sync, w1_plane, w1_scales, W1_PARTS, 0)
+        gather_scales()
+        load_part(nc.sync, w3_plane, w3_scales, W3_PARTS, 0)
+        load_part(nc.sync, w1_plane, w1_scales, W1_PARTS, 1)
+        load_w3(1)
+        for e in range(2, W3_EARLY):
             load_w1(e)
             load_w3(e)
         token_lists = [lists.tile([P, T // 16], U16, name=f"token_list{r}") for r in range(TOP)]
@@ -236,9 +238,11 @@ def tile_moe_ecr_glu_gelu_kernel(tc, x_words, x_scales, w1_words, w1_scales, w3_
             copy(out=y[:, experts[0] * C : (experts[-1] + 1) * C], in_=bank[:, : len(experts) * C])
 
         hs, quantised = {}, {}
-        for e in (0, 1, 2):
-            act = activate(e)
-            multiply(e, act, linear(e))
+        acts = {e: activate(e) for e in (0, 1)}
+        for e in (0, 1):
+            multiply(e, acts[e], linear(e))
+        act = activate(2)
+        multiply(2, act, linear(2))
         turn((0, 1), banks[6])
         act = activate(3)
         multiply(3, act, linear(3))

@@ -65,7 +65,7 @@ def tile_moe_ecr_glu_gelu_kernel(tc, x_words, x_scales, w1_words, w1_scales, w3_
             words = plane[:].rearrange("p g w -> p (g w)").bitcast(dtype).rearrange("p (a b) -> p a b", b=PAD)
             copy(out=words, in_=zeros[:].bitcast(dtype).unsqueeze(1).to_broadcast(list(words.shape)))
 
-        for plane in (w1_plane[0], w3_plane[0]):
+        for plane in (w3_plane[0], w1_plane[0]):
             clear(nc.vector.tensor_copy, plane, I32)
         y = late_pool.tile([P, SLOTS + PAD], F32, name="y")
         nc.scalar.activation(out=y[:, SLOTS:], in_=zeros[:], func=GELU)
@@ -105,20 +105,20 @@ def tile_moe_ecr_glu_gelu_kernel(tc, x_words, x_scales, w1_words, w1_scales, w3_
             for j in range(4):
                 nc.sync.dma_start(out=slot_plane[1][j:P:32, :].bitcast(I32), in_=slot_plane[0][16 + j : P : 32, :].bitcast(I32))
 
-        load_w1(0)
+        load_w3(0)
         nc.sync.dma_start(slot_list[:], offs)
         x_rows = x_scales.rearrange("s (q j) t -> j q s t", j=4)
         for j in range(4):
             nc.sync.dma_start(out=x_plane[j:P:16, :T].bitcast(I32), in_=x_rows[j].bitcast(I32))
         x_word = held.tile([P, PASSES, T], U32, name="x_word", tag="token_words", align_bytes=256)
         nc.sync.dma_start(out=x_word[:].bitcast(I32), in_=x_words.rearrange("s p t r -> p s (t r)").bitcast(I32))
-        load_w1(1)
-        load_w3(0)
-        load_part(nc.sync, w1_plane, w1_scales, W1_PARTS, 0)
-        gather_scales()
-        load_part(nc.sync, w3_plane, w3_scales, W3_PARTS, 0)
-        load_part(nc.sync, w1_plane, w1_scales, W1_PARTS, 1)
         load_w3(1)
+        load_w1(0)
+        load_part(nc.sync, w3_plane, w3_scales, W3_PARTS, 0)
+        gather_scales()
+        for g in range(2):
+            load_part(nc.sync, w1_plane, w1_scales, W1_PARTS, g)
+        load_w1(1)
         for e in range(2, W3_EARLY):
             load_w1(e)
             load_w3(e)
@@ -182,17 +182,16 @@ def tile_moe_ecr_glu_gelu_kernel(tc, x_words, x_scales, w1_words, w1_scales, w3_
         def multiply_last(e, act):
             h = held.tile([P, 2, P, 2], BF16, name="h_last")
             for m, bank in enumerate((banks[5], banks[2])):
-                for c0 in range(0, H // 2, P):
-                    for s in range(PASSES):
-                        nc.tensor.matmul_mx(
-                            out=bank[:, c0 : c0 + P],
-                            lhsT=slot_word[:, s * SLOTS + e * C : s * SLOTS + (e + 1) * C].bitcast(FP8X4),
-                            lhsT_scale=slot_plane[s][:, e * C : (e + 1) * C],
-                            rhs=w3[e][m][:, s, 2 * c0 : 2 * (c0 + P)].bitcast(FP4X4),
-                            rhs_scale=rows_of(w3_plane, W3_PARTS, e, s)[:, m * H // 2 + c0 : m * H // 2 + c0 + P],
-                            start=(s == 0),
-                            stop=(s == PASSES - 1),
-                        )
+                for s in range(PASSES):
+                    nc.tensor.matmul_mx(
+                        out=bank[:, : H // 2],
+                        lhsT=slot_word[:, s * SLOTS + e * C : s * SLOTS + (e + 1) * C].bitcast(FP8X4),
+                        lhsT_scale=slot_plane[s][:, e * C : (e + 1) * C],
+                        rhs=w3[e][m][:, s, :].bitcast(FP4X4),
+                        rhs_scale=rows_of(w3_plane, W3_PARTS, e, s)[:, m * H // 2 : (m + 1) * H // 2],
+                        start=(s == 0),
+                        stop=(s == PASSES - 1),
+                    )
                 words = slice(m * P // 2, (m + 1) * P // 2)
                 b = bank[:, : H // 2].rearrange("c (p u v) -> c u p v", u=2, v=2)
                 nc.vector.tensor_tensor(out=h[:, :, words, :], in0=b, in1=act[:, :, words, :], op=MULT)
@@ -238,9 +237,9 @@ def tile_moe_ecr_glu_gelu_kernel(tc, x_words, x_scales, w1_words, w1_scales, w3_
             copy(out=y[:, experts[0] * C : (experts[-1] + 1) * C], in_=bank[:, : len(experts) * C])
 
         hs, quantised = {}, {}
-        acts = {e: activate(e) for e in (0, 1)}
+        sums = {e: linear(e) for e in (0, 1)}
         for e in (0, 1):
-            multiply(e, acts[e], linear(e))
+            multiply(e, activate(e), sums[e])
         act = activate(2)
         multiply(2, act, linear(2))
         turn((0, 1), banks[6])
@@ -254,14 +253,14 @@ def tile_moe_ecr_glu_gelu_kernel(tc, x_words, x_scales, w1_words, w1_scales, w3_
         for e in (5, 6):
             multiply(e, acts[e], linear(e))
         multiply_last(7, acts[7])
-        turn((5,), banks[7])
+        turn((5,), banks[4])
         turn((6,), banks[0])
         turn((7,), banks[1])
         gate_column = held.tile([P, BLOCKS], F32, name="gate_column")
         nc.tensor.transpose(banks[6][:, :P], gate_rows[:], identity[:])
         nc.scalar.copy(out=gate_column[:], in_=banks[6][:, :BLOCKS])
         second((0, 1, 2, 3), banks[3], nc.scalar.copy)
-        second((4, 5, 6), banks[4], nc.vector.tensor_copy)
+        second((4, 5, 6), banks[5], nc.vector.tensor_copy)
         second((7,), banks[7], nc.scalar.copy)
 
         def picked(r, t0, t1):

from contextlib import ExitStack

import concourse.mybir as mybir
from concourse.masks import make_identity

K, T, E, C, H, N = 1024, 768, 8, 128, 512, 128
TOP = 3
PAD = 64
SLOTS = E * C
P = 128
PASSES = K // 512
FLOPS = 2 * SLOTS * (2 * K * H + H * N)

F32 = mybir.dt.float32
BF16 = mybir.dt.bfloat16
I32 = mybir.dt.int32
U32 = mybir.dt.uint32
U16 = mybir.dt.uint16
U8 = mybir.dt.uint8
FP8X4 = mybir.dt.float8_e4m3fn_x4
FP4X4 = mybir.dt.float4_e2m1fn_x4
MULT = mybir.AluOpType.mult
ADD = mybir.AluOpType.add
GELU = mybir.ActivationFunctionType.Gelu_apprx_tanh

GATHERS = ((0, 512), (512, 1024))
HALF = E // 2
W1_EARLY = 4
W1_PARTS = ((0, W1_EARLY), (W1_EARLY, E))
W3_EARLY = 5
W3_PARTS = ((0, W3_EARLY), (W3_EARLY, E))
CHUNKS = ((0, 256), (256, 512), (512, 768))
TURNED = 1
BLOCKS = T // P
A_BANK = (0, 1, 6, 0, 7, 1, 0, 1)
COPY = mybir.ActivationFunctionType.Copy


def load_scale_rows(queue, plane, rows):
    by_j = rows.rearrange("g (q j) w -> j q g w", j=4)
    for j in range(4):
        queue.dma_start(out=plane[j:P:32, :, :].bitcast(I32), in_=by_j[j].bitcast(I32))


def tile_moe_ecr_glu_gelu_kernel(tc, x_words, x_scales, w1_words, w1_scales, w3_words, w3_scales, w2_words, w2_scales, gate, offs, pos1, pos2, pos3, out):
    nc = tc.nc
    with ExitStack() as ctx:
        held = ctx.enter_context(tc.tile_pool(name="held", bufs=1))
        late_pool = ctx.enter_context(tc.tile_pool(name="late_pool", bufs=1))
        ring = ctx.enter_context(tc.tile_pool(name="ring", bufs=2))
        lists = ctx.enter_context(tc.tile_pool(name="lists", bufs=1))
        psum = ctx.enter_context(tc.psum_pool(name="psum", bufs=1))

        w1_plane = [held.tile([P, (e1 - e0) * PASSES, H], U8, name=f"w1_plane{e0}", align_bytes=256) for e0, e1 in W1_PARTS]
        w3_plane = [held.tile([P, W3_EARLY * PASSES, H], U8, name="w3_early", align_bytes=256)]
        w2_plane = held.tile([P, E, N], U8, name="w2_plane", align_bytes=256)
        x_plane = held.tile([P, 2 * T], U8, name="x_plane", tag="tokens", align_bytes=256)
        slot_plane = [held.tile([P, SLOTS], U8, name=f"slot_plane{s}", align_bytes=256) for s in range(PASSES)]
        zeros = held.tile([P, PAD], F32, name="zeros")
        nc.vector.memset(x_plane[:].bitcast(I32), 0)
        nc.vector.memset(zeros[:], 0.0)
        nc.vector.memset(slot_plane[1][:].bitcast(I32), 0)

        def clear(copy, plane, dtype):
            words = plane[:].rearrange("p g w -> p (g w)").bitcast(dtype).rearrange("p (a b) -> p a b", b=PAD)
            copy(out=words, in_=zeros[:].bitcast(dtype).unsqueeze(1).to_broadcast(list(words.shape)))

        for plane in (w3_plane[0], w1_plane[0]):
            clear(nc.vector.tensor_copy, plane, I32)
        y = late_pool.tile([P, SLOTS + PAD], F32, name="y")
        nc.scalar.activation(out=y[:, SLOTS:], in_=zeros[:], func=GELU)
        for plane in (w1_plane[1], w2_plane):
            clear(nc.scalar.copy, plane, U32)

        slot_list = held.tile([P, SLOTS // 16], U16, name="slot_list")

        w2 = [held.tile([P, HALF, 2 * N], U8, name=f"w2_{g}", align_bytes=256) for g in range(2)]
        w1, w3 = {}, {}

        def load_words(words, e, name):
            if (name, e) == ("w3", E - 1):
                halves = [held.tile([P, PASSES, H], U8, name=f"{name}_{e}_{m}", align_bytes=256) for m in range(2)]
                for m in range(2):
                    nc.sync.dma_start(out=halves[m][:].bitcast(I32), in_=words[e].rearrange("s p b -> p s b")[:, :, m * H : (m + 1) * H].bitcast(I32))
                return halves
            tile = held.tile([P, PASSES, 2 * H], U8, name=f"{name}_{e}", align_bytes=256)
            nc.sync.dma_start(out=tile[:].bitcast(I32), in_=words[e].rearrange("s p b -> p s b").bitcast(I32))
            return [tile[:, s, :] for s in range(PASSES)]

        def load_w1(e):
            w1[e] = load_words(w1_words, e, "w1")

        def load_w3(e):
            w3[e] = load_words(w3_words, e, "w3")

        def load_part(queue, planes, scales, parts, g):
            load_scale_rows(queue, planes[g], scales[parts[g][0] : parts[g][1]].rearrange("e s q i -> (e s) q i"))

        def rows_of(planes, parts, e, s):
            g = int(e >= parts[1][0])
            return planes[g][:, (e - parts[g][0]) * PASSES + s, :]

        def gather_scales():
            nc.vector.tensor_copy(slot_plane[0][:], x_plane[:].indirect(slot_list[:]))
            for j in range(4):
                nc.sync.dma_start(out=slot_plane[1][j:P:32, :].bitcast(I32), in_=slot_plane[0][16 + j : P : 32, :].bitcast(I32))

        load_w3(0)
        nc.sync.dma_start(slot_list[:], offs)
        x_rows = x_scales.rearrange("s (q j) t -> j q s t", j=4)
        for j in range(4):
            nc.sync.dma_start(out=x_plane[j:P:16, :T].bitcast(I32), in_=x_rows[j].bitcast(I32))
        x_word = held.tile([P, PASSES, T], U32, name="x_word", tag="token_words", align_bytes=256)
        nc.sync.dma_start(out=x_word[:].bitcast(I32), in_=x_words.rearrange("s p t r -> p s (t r)").bitcast(I32))
        load_w3(1)
        load_w1(0)
        load_part(nc.sync, w3_plane, w3_scales, W3_PARTS, 0)
        gather_scales()
        for g in range(2):
            load_part(nc.sync, w1_plane, w1_scales, W1_PARTS, g)
        load_w1(1)
        for e in range(2, W3_EARLY):
            load_w1(e)
            load_w3(e)
        token_lists = [lists.tile([P, T // 16], U16, name=f"token_list{r}") for r in range(TOP)]
        for e, token_list, pos in zip(range(W3_EARLY, E), token_lists, (pos1, pos2, pos3)):
            load_w1(e)
            nc.sync.dma_start(token_list[:], pos)
        for e in range(W3_EARLY, E):
            load_w3(e)
        gate_rows = held.tile([P, P], F32, name="gate_rows", align_bytes=256)
        nc.sync.dma_start(out=gate_rows[:], in_=gate[2].rearrange("n (b t) -> (n b) t", t=P)[:P])
        load_scale_rows(nc.sync, w2_plane, w2_scales.rearrange("e s q n -> (e s) q n"))
        for g in range(2):
            nc.sync.dma_start(out=w2[g][:].bitcast(I32), in_=w2_words[g * HALF : (g + 1) * HALF].rearrange("e s p b -> p (e s) b").bitcast(I32))

        split = CHUNKS[TURNED][0]
        gates = {}

        def load_gate(r, t0, t1):
            gates[r, t0] = held.tile([P, t1 - t0], F32, name=f"gate{r}_{t0}", align_bytes=256)
            nc.sync.dma_start(out=gates[r, t0][:], in_=gate[r][:, t0:t1])

        load_gate(1, 0, split)
        load_gate(1, split, T)
        load_gate(0, split, T)
        load_gate(0, 0, split)

        identity = held.tile([P, P], F32, name="identity")
        make_identity(nc, identity[:])

        banks = [psum.tile([P, H], F32, name=f"bank{b}") for b in range(8)]

        slot_word = held.tile([P, PASSES * SLOTS], U32, name="slot_word", tag="tokens", align_bytes=256)
        for c0, c1 in GATHERS:
            for s in range(PASSES):
                nc.vector.tensor_copy(slot_word[:, s * SLOTS + c0 : s * SLOTS + c1], x_word[:, s, :].indirect(slot_list[:, c0 // 16 : c1 // 16]))

        w3_plane.append(held.tile([P, (E - W3_EARLY) * PASSES, H], U8, name="w3_late", tag="token_words", align_bytes=256))
        load_part(nc.gpsimd, w3_plane, w3_scales, W3_PARTS, 1)

        def first_product(e, words, planes, parts, acc):
            slots = slice(e * C, (e + 1) * C)
            for s in range(PASSES):
                nc.tensor.matmul_mx(
                    out=acc[:],
                    lhsT=slot_word[:, s * SLOTS + e * C : s * SLOTS + (e + 1) * C].bitcast(FP8X4),
                    lhsT_scale=slot_plane[s][:, slots],
                    rhs=words[s].bitcast(FP4X4),
                    rhs_scale=rows_of(planes, parts, e, s),
                    start=(s == 0),
                    stop=(s == PASSES - 1),
                )
            return acc[:].rearrange("c (p u v) -> c u p v", u=2, v=2)

        def activate(e):
            a = first_product(e, w1[e], w1_plane, W1_PARTS, banks[A_BANK[e]])
            act = ring.tile([P, 2, P, 2], F32, name="act", bufs=8)
            nc.scalar.activation(out=act[:], in_=a, func=GELU)
            return act

        def multiply_last(e, act):
            h = held.tile([P, 2, P, 2], BF16, name="h_last")
            for m, bank in enumerate((banks[5], banks[2])):
                for s in range(PASSES):
                    nc.tensor.matmul_mx(
                        out=bank[:, : H // 2],
                        lhsT=slot_word[:, s * SLOTS + e * C : s * SLOTS + (e + 1) * C].bitcast(FP8X4),
                        lhsT_scale=slot_plane[s][:, e * C : (e + 1) * C],
                        rhs=w3[e][m][:, s, :].bitcast(FP4X4),
                        rhs_scale=rows_of(w3_plane, W3_PARTS, e, s)[:, m * H // 2 : (m + 1) * H // 2],
                        start=(s == 0),
                        stop=(s == PASSES - 1),
                    )
                words = slice(m * P // 2, (m + 1) * P // 2)
                b = bank[:, : H // 2].rearrange("c (p u v) -> c u p v", u=2, v=2)
                nc.vector.tensor_tensor(out=h[:, :, words, :], in0=b, in1=act[:, :, words, :], op=MULT)
            hs[e] = [h[:, u] for u in range(2)]

        def linear(e):
            return first_product(e, w3[e], w3_plane, W3_PARTS, banks[2 + e % 4])

        def multiply(e, act, b):
            h = ring.tile([P, 2, P, 2], BF16, name="h", bufs=8)
            nc.vector.tensor_tensor(out=h[:], in0=b, in1=act[:], op=MULT)
            hs[e] = [h[:, u] for u in range(2)]

        def turn(group, bank):
            width = len(group) * C
            turned = bank[:, : 2 * width].rearrange("p (m u c) -> p m u c", u=2, c=C)
            for m, e in enumerate(group):
                for u in range(2):
                    nc.tensor.transpose(turned[:, m, u, :], hs[e][u].rearrange("c p v -> c (p v)").bitcast(F32), identity[:])
            grouped = ring.tile([P, 4 * width], BF16, name="grouped", bufs=3, align_bytes=256)
            nc.scalar.copy(
                out=grouped[:].bitcast(F32).rearrange("p (m c u) -> p m c u", c=C, u=2),
                in_=turned.rearrange("p m u c -> p m c u"),
            )
            h_word = held.tile([P, width], U32, name=f"h_word{group[0]}", align_bytes=256)
            h_plane = held.tile([P, width], U8, name=f"h_plane{group[0]}", align_bytes=256)
            nc.vector.quantize_mx(out=h_word[:].bitcast(FP8X4), scales=h_plane[:], in_=grouped[:])
            for m, e in enumerate(group):
                quantised[e] = (h_word[:, m * C : (m + 1) * C], h_plane[:, m * C : (m + 1) * C])

        def second(experts, bank, copy):
            for m, e in enumerate(experts):
                h_word, h_plane = quantised[e]
                nc.tensor.matmul_mx(
                    out=bank[:, m * C : (m + 1) * C],
                    lhsT=w2[e // HALF][:, e % HALF, :].bitcast(FP4X4),
                    lhsT_scale=w2_plane[:, e, :],
                    rhs=h_word.bitcast(FP8X4),
                    rhs_scale=h_plane,
                    start=True,
                    stop=True,
                )
            copy(out=y[:, experts[0] * C : (experts[-1] + 1) * C], in_=bank[:, : len(experts) * C])

        hs, quantised = {}, {}
        sums = {e: linear(e) for e in (0, 1)}
        for e in (0, 1):
            multiply(e, activate(e), sums[e])
        act = activate(2)
        multiply(2, act, linear(2))
        turn((0, 1), banks[6])
        act = activate(3)
        multiply(3, act, linear(3))
        act = activate(4)
        multiply(4, act, linear(4))
        turn((2, 3), banks[7])
        acts = {e: activate(e) for e in (5, 6, 7)}
        turn((4,), banks[6])
        for e in (5, 6):
            multiply(e, acts[e], linear(e))
        multiply_last(7, acts[7])
        turn((5,), banks[4])
        turn((6,), banks[0])
        turn((7,), banks[1])
        gate_column = held.tile([P, BLOCKS], F32, name="gate_column")
        nc.tensor.transpose(banks[6][:, :P], gate_rows[:], identity[:])
        nc.scalar.copy(out=gate_column[:], in_=banks[6][:, :BLOCKS])
        second((0, 1, 2, 3), banks[3], nc.scalar.copy)
        second((4, 5, 6), banks[5], nc.vector.tensor_copy)
        second((7,), banks[7], nc.scalar.copy)

        def picked(r, t0, t1):
            return y[:].indirect(token_lists[r][:, t0 // 16 : t1 // 16])

        def gated(r, t0, t1):
            term = held.tile([P, t1 - t0], F32, name=f"term{r}_{t0}")
            nc.vector.tensor_tensor(term[:], picked(r, t0, t1), gates[r, t0][:], MULT)
            return term

        def by_token(term, bank):
            for b0 in range(0, term.shape[1], P):
                nc.tensor.transpose(bank[:, b0 : b0 + P], term[:, b0 : b0 + P], identity[:])
            return bank[:, : term.shape[1]]

        third, second_turned = [], []
        for c, (t0, t1) in enumerate(CHUNKS):
            plain = held.tile([P, t1 - t0], F32, name=f"plain{c}")
            nc.scalar.activation(out=plain[:], in_=picked(2, t0, t1), func=COPY)
            third.append(by_token(plain, banks[1 + c]))
            if c < TURNED:
                second_turned.append(by_token(gated(1, t0, t1), banks[7 * c]))
        for c, (t0, t1) in enumerate(CHUNKS):
            parts = [held.tile([P, t1 - t0], F32, name=f"third{c}")]
            for b0 in range(0, t1 - t0, P):
                k = (t0 + b0) // P
                nc.scalar.activation(out=parts[0][:, b0 : b0 + P], in_=third[c][:, b0 : b0 + P], func=COPY, scale=gate_column[:, k : k + 1])
            if c < TURNED:
                parts.append(held.tile([P, t1 - t0], F32, name=f"second{c}"))
                nc.scalar.copy(out=parts[1][:], in_=second_turned[c])
            for b0 in range(0, t1 - t0, P):
                for n, part in enumerate(parts):
                    nc.tensor.matmul(banks[4 + c][:, b0 : b0 + P], lhsT=part[:, b0 : b0 + P], rhs=identity[:], is_transpose=True, start=(n == 0), stop=(n == len(parts) - 1))
        late2 = gated(1, split, T)
        late1 = gated(0, split, T)
        early1 = gated(0, 0, split)
        late = held.tile([P, T - split], F32, name="late")
        nc.vector.tensor_tensor(late[:], late2[:], late1[:], ADD)
        for c, (t0, t1) in enumerate(CHUNKS):
            term = early1[:, t0:t1] if c < TURNED else late[:, t0 - split : t1 - split]
            result = held.tile([P, t1 - t0], F32, name=f"result{c}", align_bytes=256)
            nc.vector.tensor_tensor(result[:], banks[4 + c][:, : t1 - t0], term, ADD)
            nc.sync.dma_start(out=out[:, t0:t1], in_=result[:])
